import numpy as np
import ml_dtypes


def mxq(x, axis, fmt="e4m3"):
    dtype, down = {"e4m3": (ml_dtypes.float8_e4m3fn, 7), "e5m2": (ml_dtypes.float8_e5m2, 14)}[fmt]
    v = np.moveaxis(np.asarray(x, np.float32).astype(ml_dtypes.bfloat16).astype(np.float64), axis, -1)
    blocks = v.reshape(v.shape[:-1] + (-1, 32))
    amax = np.abs(blocks).max(-1, keepdims=True)
    byte = np.maximum(np.where(amax > 0, np.frexp(amax)[1] - 1 + 127, 0) - down, 1)
    scale = np.exp2(byte - 127.0)
    codes = (blocks / scale).astype(np.float32).astype(dtype).astype(np.float64)
    return np.moveaxis((codes * scale).reshape(v.shape), -1, axis)


WIDE = False


def mx_kscale(k):
    if not WIDE:
        return np.ones(k)
    levels = np.array([10, -10, 5, -5, 0])
    if k % 512:
        return np.exp2(np.random.permutation(np.resize(levels, k // 32))).repeat(32)
    a = np.empty((k // 512, 16))
    for p in range(k // 512):
        a[p, :8] = np.random.permutation(np.resize(levels, 8))
        for g in range(8):
            far = levels[np.abs(levels - a[p, g]) >= 10]
            a[p, g + 8] = far[np.random.randint(len(far))]
    return np.exp2(a.ravel()).repeat(32)


def f64(x):
    return np.asarray(x).astype(np.float64)


def striped(idx):
    return np.tile(idx.reshape(-1, 16).T, (8, 1)).astype(np.uint16)


def unstriped(offs):
    return offs[:16].T.reshape(-1).astype(np.int64)


def silu(v):
    return v / (1.0 + np.exp(-np.maximum(v, -700.0)))


K, T, D, S, V, H, N = 1024, 2048, 8, 4096, 512, 1024, 128


def setup_inputs():
    n = np.random.standard_normal
    s = mx_kscale(K)[:, None]
    u = mx_kscale(H)
    return {
        "xT": (n((K, T)) * s).astype(np.float32),
        "w1": (n((K, H)) / np.sqrt(K) / s * u).astype(np.float32),
        "w2": (n((H, N)) / np.sqrt(H) / u[:, None]).astype(np.float32),
        "offs": striped(np.concatenate([np.random.permutation(T)[:V] for _ in range(D)])),
    }


def reference(xT, w1, w2, offs):
    idx = unstriped(offs)
    x = np.empty((K, V))
    for l in range(D):
        r = l // 4 * (4 * K // D) + l % 4 + 4 * np.arange(K // D)
        x[r] = f64(xT)[r][:, idx[l * V:(l + 1) * V]]
    xq = mxq(x, 0, "e4m3")
    h = silu(mxq(f64(w1), 0, "e4m3").T @ xq)
    return mxq(f64(w2), 0, "e4m3").T @ mxq(h, 0, "e4m3")

@@ -1,0 +1,188 @@
+from contextlib import ExitStack
+
+import concourse.mybir as mybir
+
+K, T, LEVELS, V, H, N = 1024, 2048, 8, 512, 1024, 128
+FLOPS = 2 * K * H * V + 2 * H * N * V
+
+F32 = mybir.dt.float32
+BF16 = mybir.dt.bfloat16
+U32 = mybir.dt.uint32
+U16 = mybir.dt.uint16
+U8 = mybir.dt.uint8
+FP8X4 = mybir.dt.float8_e4m3fn_x4
+SILU = mybir.ActivationFunctionType.Silu
+
+P = 128
+PACK = 4
+K_PASS = P * PACK
+PASSES = K // K_PASS
+HALVES = H // K_PASS
+HALF_COLS = K_PASS // 2
+POINTS = 128
+CHUNKS = V // POINTS
+LIST_COLS = V // 16
+WARM_UPS = 4
+EARLY_STORED = 2
+
+
+def tile_picked_grid_mlp_silu_sub_l_kernel(tc, xT, w1, w2, offs, out):
+    nc = tc.nc
+    with ExitStack() as ctx:
+        keep = ctx.enter_context(tc.tile_pool(name="keep", bufs=1))
+        banks = ctx.enter_context(tc.psum_pool(name="banks", bufs=8))
+
+        table_loader = keep.tile([P, 2], F32, name="table_loader")
+        nc.vector.memset(table_loader[:], 0.0)
+        nc.scalar.activation(table_loader[:, 1:2], table_loader[:, 0:1], SILU)
+
+        w1_rows = [w1[k * K_PASS:(k + 1) * K_PASS, :].rearrange("(p j) w -> p j w", j=PACK) for k in range(PASSES)]
+        xT_rows = [xT[g * K_PASS:(g + 1) * K_PASS, :].rearrange("(f j) w -> f j w", j=PACK) for g in range(PASSES)]
+
+        offsets = keep.tile([P, LEVELS * LIST_COLS], U16, name="offsets")
+        nc.sync.dma_start(offsets[:], offs)
+
+        w1_first = keep.tile([P, PACK, H], F32, name="w1_first")
+        nc.sync.dma_start(out=w1_first[:], in_=w1_rows[0])
+        w1_second = [keep.tile([P, PACK, K_PASS], F32, name=f"w1_second{c}") for c in range(HALVES)]
+        nc.sync.dma_start(out=w1_second[0][:], in_=w1_rows[1][:, :, 0:K_PASS])
+
+        tables = {}
+
+        def load_tables(first, count):
+            g, t = first // PACK, first % PACK
+            tile = keep.tile([P, count, T], F32, name=f"tables{first}")
+            nc.sync.dma_start(out=tile[:], in_=xT_rows[g][:, t:t + count, :])
+            for i in range(count):
+                tables[first + i] = tile[:, i, :]
+
+        load_tables(4, 2)
+        for level in (0, 1, 2, 3, 6, 7):
+            load_tables(level, 1)
+
+        for a in range(0, K_PASS, HALF_COLS):
+            nc.sync.dma_start(out=w1_second[1][:, :, a:a + HALF_COLS],
+                              in_=w1_rows[1][:, :, K_PASS + a:K_PASS + a + HALF_COLS])
+        w2_raw = keep.tile([P, HALVES, PACK, N], F32, name="w2_raw")
+        nc.sync.dma_start(out=w2_raw[:], in_=w2.rearrange("(c p j) n -> p c j n", p=P, j=PACK))
+
+        def quantize(codes, scales, grouped):
+            nc.vector.quantize_mx(out=codes.bitcast(FP8X4), scales=scales, in_=grouped)
+
+        w1_codes = [[keep.tile([P, K_PASS], U32, name=f"w1_codes{k}{c}", align_bytes=64) for c in range(HALVES)]
+                    for k in range(PASSES)]
+        w1_scales = [[keep.tile([P, K_PASS], U8, name=f"w1_scales{k}{c}", align_bytes=64) for c in range(HALVES)]
+                     for k in range(PASSES)]
+
+        def prepare_w1(k, c, raw, parts=1, copy=nc.vector.tensor_copy):
+            grouped = keep.tile([P, K_PASS * PACK], BF16, name=f"w1_grouped{k}{c}", align_bytes=64)
+            for part in range(parts):
+                m = slice(part * P // parts, (part + 1) * P // parts)
+                copy(
+                    out=grouped[:].rearrange("p (t m j) -> p m t j", t=PACK, j=PACK)[:, m, :, :],
+                    in_=raw.rearrange("p j (m t) -> p m t j", t=PACK)[:, m, :, :],
+                )
+            quantize(w1_codes[k][c][:], w1_scales[k][c][:], grouped[:])
+
+        x_grouped = [keep.tile([P, V, PACK], BF16, name=f"x_grouped{g}", align_bytes=64) for g in range(PASSES)]
+        x_codes = [keep.tile([P, V], U32, name=f"x_codes{g}", align_bytes=64) for g in range(PASSES)]
+        x_scales = [keep.tile([P, V], U8, name=f"x_scales{g}", align_bytes=64) for g in range(PASSES)]
+
+        def look_up(level, parts=1):
+            g, t = level // PACK, level % PACK
+            for part in range(parts):
+                v0, v1 = part * V // parts, (part + 1) * V // parts
+                first = level * LIST_COLS
+                nc.vector.tensor_copy(
+                    x_grouped[g][:, v0:v1, t],
+                    tables[level].indirect(offsets[:, first + v0 // 16:first + v1 // 16]),
+                )
+
+        def quantize_x(g, parts=1):
+            for part in range(parts):
+                v = slice(part * V // parts, (part + 1) * V // parts)
+                quantize(x_codes[g][:, v], x_scales[g][:, v], x_grouped[g][:, v, :].rearrange("p v t -> p (v t)"))
+
+        w2_grouped = keep.tile([P, HALVES, N, PACK], BF16, name="w2_grouped", align_bytes=64)
+        w2_codes = keep.tile([P, HALVES, N], U32, name="w2_codes", align_bytes=64)
+        w2_scales = keep.tile([P, HALVES, N], U8, name="w2_scales", align_bytes=64)
+
+        def prepare_w2():
+            nc.vector.tensor_copy(w2_grouped[:], w2_raw[:].rearrange("p c j n -> p c n j"))
+            quantize(w2_codes[:].rearrange("p c n -> p (c n)"), w2_scales[:].rearrange("p c n -> p (c n)"),
+                     w2_grouped[:].rearrange("p c n j -> p (c n j)"))
+
+        def warm_up():
+            spare = banks.tile([P, V], F32, name="spare", tag="bank")
+            for turn in range(WARM_UPS):
+                nc.tensor.matmul_mx(
+                    out=spare[:],
+                    lhsT=w1_codes[0][0][:, 0:P].bitcast(FP8X4),
+                    lhsT_scale=w1_scales[0][0][:, 0:P],
+                    rhs=x_codes[0][:].bitcast(FP8X4),
+                    rhs_scale=x_scales[0][:],
+                    start=True,
+                    stop=True,
+                )
+
+        h = [keep.tile([P, HALVES, POINTS, PACK], BF16, name=f"h{n}", align_bytes=64) for n in range(CHUNKS)]
+        h_codes = [keep.tile([P, HALVES, POINTS], U32, name=f"h_codes{n}", align_bytes=64) for n in range(CHUNKS)]
+        h_scales = [keep.tile([P, HALVES, POINTS], U8, name=f"h_scales{n}", align_bytes=64) for n in range(CHUNKS)]
+
+        def first_layer(c):
+            for n in range(CHUNKS):
+                v = slice(n * POINTS, (n + 1) * POINTS)
+                bank = banks.tile([P, PACK, POINTS], F32, name="bank", tag="bank")
+                for t in range(PACK):
+                    channels = slice(t * P, (t + 1) * P)
+                    for k in range(PASSES):
+                        nc.tensor.matmul_mx(
+                            out=bank[:, t, :],
+                            lhsT=w1_codes[k][c][:, channels].bitcast(FP8X4),
+                            lhsT_scale=w1_scales[k][c][:, channels],
+                            rhs=x_codes[k][:, v].bitcast(FP8X4),
+                            rhs_scale=x_scales[k][:, v],
+                            start=(k == 0),
+                            stop=(k == PASSES - 1),
+                        )
+                nc.scalar.activation(h[n][:, c], bank[:].rearrange("p t v -> p v t"), SILU)
+
+        prepare_w1(0, 0, w1_first[:, :, 0:K_PASS], copy=nc.scalar.copy)
+        prepare_w1(0, 1, w1_first[:, :, K_PASS:H])
+        prepare_w1(1, 0, w1_second[0][:])
+        for level in (4, 5, 0, 1, 2, 3):
+            look_up(level)
+        quantize_x(0)
+        warm_up()
+        look_up(6)
+        look_up(7, parts=2)
+        quantize_x(1, parts=2)
+        prepare_w1(1, 1, w1_second[1][:], parts=2)
+        prepare_w2()
+        for c in range(HALVES):
+            first_layer(c)
+
+        result = keep.tile([P, CHUNKS, POINTS], F32, name="result", align_bytes=64)
+        for n in range(CHUNKS):
+            if n < CHUNKS // 2:
+                quantize(h_codes[n][:].rearrange("p c v -> p (c v)"), h_scales[n][:].rearrange("p c v -> p (c v)"),
+                         h[n][:].rearrange("p c v t -> p (c v t)"))
+            else:
+                for c in range(HALVES):
+                    quantize(h_codes[n][:, c], h_scales[n][:, c], h[n][:, c].rearrange("p v t -> p (v t)"))
+            bank = banks.tile([P, PACK, POINTS], F32, name="out_bank", tag="bank")
+            for c in range(HALVES):
+                nc.tensor.matmul_mx(
+                    out=bank[:, 0, :],
+                    lhsT=w2_codes[:, c, :].bitcast(FP8X4),
+                    lhsT_scale=w2_scales[:, c, :],
+                    rhs=h_codes[n][:, c, :].bitcast(FP8X4),
+                    rhs_scale=h_scales[n][:, c, :],
+                    start=(c == 0),
+                    stop=(c == HALVES - 1),
+                )
+            nc.vector.tensor_copy(result[:, n, :], bank[:, 0, :])
+            if n >= EARLY_STORED - 1:
+                first = 0 if n == EARLY_STORED - 1 else n
+                nc.sync.dma_start(out=out[:, first * POINTS:(n + 1) * POINTS],
+                                  in_=result[:, first:n + 1, :].rearrange("p n v -> p (n v)"))

@@ -18,12 +18,9 @@ PACK = 4
 K_PASS = P * PACK
 PASSES = K // K_PASS
 HALVES = H // K_PASS
-HALF_COLS = K_PASS // 2
 POINTS = 128
 CHUNKS = V // POINTS
 LIST_COLS = V // 16
-WARM_UPS = 4
-EARLY_STORED = 2
 
 
 def tile_picked_grid_mlp_silu_sub_l_kernel(tc, xT, w1, w2, offs, out):
@@ -40,13 +37,6 @@ def tile_picked_grid_mlp_silu_sub_l_kernel(tc, xT, w1, w2, offs, out):
         xT_rows = [xT[g * K_PASS:(g + 1) * K_PASS, :].rearrange("(f j) w -> f j w", j=PACK) for g in range(PASSES)]
 
         offsets = keep.tile([P, LEVELS * LIST_COLS], U16, name="offsets")
-        nc.sync.dma_start(offsets[:], offs)
-
-        w1_first = keep.tile([P, PACK, H], F32, name="w1_first")
-        nc.sync.dma_start(out=w1_first[:], in_=w1_rows[0])
-        w1_second = [keep.tile([P, PACK, K_PASS], F32, name=f"w1_second{c}") for c in range(HALVES)]
-        nc.sync.dma_start(out=w1_second[0][:], in_=w1_rows[1][:, :, 0:K_PASS])
-
         tables = {}
 
         def load_tables(first, count):
@@ -56,33 +46,42 @@ def tile_picked_grid_mlp_silu_sub_l_kernel(tc, xT, w1, w2, offs, out):
             for i in range(count):
                 tables[first + i] = tile[:, i, :]
 
-        load_tables(4, 2)
-        for level in (0, 1, 2, 3, 6, 7):
-            load_tables(level, 1)
+        def load_w1(k, a, b):
+            tile = keep.tile([P, PACK, b - a], F32, name=f"w1_raw{k}_{a}")
+            nc.sync.dma_start(out=tile[:], in_=w1_rows[k][:, :, a:b])
+            return tile
 
-        for a in range(0, K_PASS, HALF_COLS):
-            nc.sync.dma_start(out=w1_second[1][:, :, a:a + HALF_COLS],
-                              in_=w1_rows[1][:, :, K_PASS + a:K_PASS + a + HALF_COLS])
         w2_raw = keep.tile([P, HALVES, PACK, N], F32, name="w2_raw")
-        nc.sync.dma_start(out=w2_raw[:], in_=w2.rearrange("(c p j) n -> p c j n", p=P, j=PACK))
+
+        def load_w2():
+            nc.sync.dma_start(out=w2_raw[:], in_=w2.rearrange("(c p j) n -> p c j n", p=P, j=PACK))
+
+        nc.sync.dma_start(offsets[:], offs)
+        load_tables(4, 3)
+        w1_first = load_w1(0, 0, H)
+        for level in (0, 1, 2, 3, 7):
+            load_tables(level, 1)
+        late = [load_w1(1, a, a + 256) for a in range(0, H, 256)]
+        load_w2()
 
         def quantize(codes, scales, grouped):
             nc.vector.quantize_mx(out=codes.bitcast(FP8X4), scales=scales, in_=grouped)
 
+        w1_grouped = [[keep.tile([P, K_PASS * PACK], BF16, name=f"w1_grouped{k}{c}", align_bytes=64)
+                       for c in range(HALVES)] for k in range(PASSES)]
         w1_codes = [[keep.tile([P, K_PASS], U32, name=f"w1_codes{k}{c}", align_bytes=64) for c in range(HALVES)]
                     for k in range(PASSES)]
         w1_scales = [[keep.tile([P, K_PASS], U8, name=f"w1_scales{k}{c}", align_bytes=64) for c in range(HALVES)]
                      for k in range(PASSES)]
 
-        def prepare_w1(k, c, raw, parts=1, copy=nc.vector.tensor_copy):
-            grouped = keep.tile([P, K_PASS * PACK], BF16, name=f"w1_grouped{k}{c}", align_bytes=64)
-            for part in range(parts):
-                m = slice(part * P // parts, (part + 1) * P // parts)
-                copy(
-                    out=grouped[:].rearrange("p (t m j) -> p m t j", t=PACK, j=PACK)[:, m, :, :],
-                    in_=raw.rearrange("p j (m t) -> p m t j", t=PACK)[:, m, :, :],
-                )
-            quantize(w1_codes[k][c][:], w1_scales[k][c][:], grouped[:])
+        def cast_w1(k, c, raw, m0, m1, copy, ts=slice(0, PACK)):
+            copy(
+                out=w1_grouped[k][c][:].rearrange("p (t m j) -> p m t j", t=PACK, j=PACK)[:, m0:m1, ts, :],
+                in_=raw.rearrange("p j (m t) -> p m t j", t=PACK)[:, :, ts, :],
+            )
+
+        def quantize_w1(k, c, a=0, b=K_PASS):
+            quantize(w1_codes[k][c][:, a:b], w1_scales[k][c][:, a:b], w1_grouped[k][c][:, PACK * a:PACK * b])
 
         x_grouped = [keep.tile([P, V, PACK], BF16, name=f"x_grouped{g}", align_bytes=64) for g in range(PASSES)]
         x_codes = [keep.tile([P, V], U32, name=f"x_codes{g}", align_bytes=64) for g in range(PASSES)]
@@ -112,77 +111,101 @@ def tile_picked_grid_mlp_silu_sub_l_kernel(tc, xT, w1, w2, offs, out):
             quantize(w2_codes[:].rearrange("p c n -> p (c n)"), w2_scales[:].rearrange("p c n -> p (c n)"),
                      w2_grouped[:].rearrange("p c n j -> p (c n j)"))
 
-        def warm_up():
-            spare = banks.tile([P, V], F32, name="spare", tag="bank")
-            for turn in range(WARM_UPS):
+        h = [keep.tile([P, V, PACK], BF16, name=f"h{c}", align_bytes=64) for c in range(HALVES)]
+        h_codes = [keep.tile([P, V], U32, name=f"h_codes{c}", align_bytes=64) for c in range(HALVES)]
+        h_scales = [keep.tile([P, V], U8, name=f"h_scales{c}", align_bytes=64) for c in range(HALVES)]
+        sums = {}
+
+        def first_layer(k, c, n, first):
+            v = slice(n * POINTS, (n + 1) * POINTS)
+            if first:
+                sums[c, n] = banks.tile([P, PACK, POINTS], F32, name="bank", tag="bank")
+            for t in range(PACK):
+                channels = slice(t * P, (t + 1) * P)
                 nc.tensor.matmul_mx(
-                    out=spare[:],
-                    lhsT=w1_codes[0][0][:, 0:P].bitcast(FP8X4),
-                    lhsT_scale=w1_scales[0][0][:, 0:P],
-                    rhs=x_codes[0][:].bitcast(FP8X4),
-                    rhs_scale=x_scales[0][:],
-                    start=True,
-                    stop=True,
+                    out=sums[c, n][:, t, :],
+                    lhsT=w1_codes[k][c][:, channels].bitcast(FP8X4),
+                    lhsT_scale=w1_scales[k][c][:, channels],
+                    rhs=x_codes[k][:, v].bitcast(FP8X4),
+                    rhs_scale=x_scales[k][:, v],
+                    start=(first and t == 0),
+                    stop=(not first and t == PACK - 1),
                 )
 
-        h = [keep.tile([P, HALVES, POINTS, PACK], BF16, name=f"h{n}", align_bytes=64) for n in range(CHUNKS)]
-        h_codes = [keep.tile([P, HALVES, POINTS], U32, name=f"h_codes{n}", align_bytes=64) for n in range(CHUNKS)]
-        h_scales = [keep.tile([P, HALVES, POINTS], U8, name=f"h_scales{n}", align_bytes=64) for n in range(CHUNKS)]
+        def activate(c, n):
+            v = slice(n * POINTS, (n + 1) * POINTS)
+            nc.scalar.activation(h[c][:, v, :], sums[c, n][:].rearrange("p t v -> p v t"), SILU)
 
-        def first_layer(c):
-            for n in range(CHUNKS):
-                v = slice(n * POINTS, (n + 1) * POINTS)
-                bank = banks.tile([P, PACK, POINTS], F32, name="bank", tag="bank")
-                for t in range(PACK):
-                    channels = slice(t * P, (t + 1) * P)
-                    for k in range(PASSES):
-                        nc.tensor.matmul_mx(
-                            out=bank[:, t, :],
-                            lhsT=w1_codes[k][c][:, channels].bitcast(FP8X4),
-                            lhsT_scale=w1_scales[k][c][:, channels],
-                            rhs=x_codes[k][:, v].bitcast(FP8X4),
-                            rhs_scale=x_scales[k][:, v],
-                            start=(k == 0),
-                            stop=(k == PASSES - 1),
-                        )
-                nc.scalar.activation(h[n][:, c], bank[:].rearrange("p t v -> p v t"), SILU)
+        def quantize_h(c, a, b):
+            v = slice(a * POINTS, b * POINTS)
+            quantize(h_codes[c][:, v], h_scales[c][:, v], h[c][:, v, :].rearrange("p v t -> p (v t)"))
 
-        prepare_w1(0, 0, w1_first[:, :, 0:K_PASS], copy=nc.scalar.copy)
-        prepare_w1(0, 1, w1_first[:, :, K_PASS:H])
-        prepare_w1(1, 0, w1_second[0][:])
-        for level in (4, 5, 0, 1, 2, 3):
+        outs = {}
+
+        def second_layer(c, n):
+            v = slice(n * POINTS, (n + 1) * POINTS)
+            if c == 0:
+                outs[n] = banks.tile([P, PACK, POINTS], F32, name="out_bank", tag="bank")
+            nc.tensor.matmul_mx(
+                out=outs[n][:, 0, :],
+                lhsT=w2_codes[:, c, :].bitcast(FP8X4),
+                lhsT_scale=w2_scales[:, c, :],
+                rhs=h_codes[c][:, v].bitcast(FP8X4),
+                rhs_scale=h_scales[c][:, v],
+                start=(c == 0),
+                stop=(c == HALVES - 1),
+            )
+
+        result = keep.tile([P, V], F32, name="result", align_bytes=64)
+
+        def copy_out(n, copy):
+            copy(result[:, n * POINTS:(n + 1) * POINTS], outs[n][:, 0, :])
+
+        def store(a, b, queue):
+            queue.dma_start(out=out[:, a * POINTS:b * POINTS], in_=result[:, a * POINTS:b * POINTS])
+
+        vcopy, scopy = nc.vector.tensor_copy, nc.scalar.copy
+
+        def quantize_w1_part(k, c, part):
+            for t in range(PACK):
+                quantize_w1(k, c, t * P + part * 64, t * P + part * 64 + 64)
+
+        for level in (4, 5, 6):
+            look_up(level)
+        for c in range(HALVES):
+            cast_w1(0, c, w1_first[:, :, c * K_PASS:(c + 1) * K_PASS], 0, P, scopy)
+            quantize_w1(0, c)
+        for level in (0, 1, 2, 3):
             look_up(level)
         quantize_x(0)
-        warm_up()
-        look_up(6)
-        look_up(7, parts=2)
-        quantize_x(1, parts=2)
-        prepare_w1(1, 1, w1_second[1][:], parts=2)
-        prepare_w2()
         for c in range(HALVES):
-            first_layer(c)
-
-        result = keep.tile([P, CHUNKS, POINTS], F32, name="result", align_bytes=64)
+            for n in range(CHUNKS):
+                first_layer(0, c, n, True)
+        look_up(7)
+        quantize_x(1)
+        cast_w1(1, 0, late[0][:], 0, 64, scopy)
+        cast_w1(1, 0, late[1][:], 64, P, vcopy)
+        quantize_w1_part(1, 0, 0)
+        quantize_w1_part(1, 0, 1)
         for n in range(CHUNKS):
-            if n < CHUNKS // 2:
-                quantize(h_codes[n][:].rearrange("p c v -> p (c v)"), h_scales[n][:].rearrange("p c v -> p (c v)"),
-                         h[n][:].rearrange("p c v t -> p (c v t)"))
-            else:
-                for c in range(HALVES):
-                    quantize(h_codes[n][:, c], h_scales[n][:, c], h[n][:, c].rearrange("p v t -> p (v t)"))
-            bank = banks.tile([P, PACK, POINTS], F32, name="out_bank", tag="bank")
-            for c in range(HALVES):
-                nc.tensor.matmul_mx(
-                    out=bank[:, 0, :],
-                    lhsT=w2_codes[:, c, :].bitcast(FP8X4),
-                    lhsT_scale=w2_scales[:, c, :],
-                    rhs=h_codes[n][:, c, :].bitcast(FP8X4),
-                    rhs_scale=h_scales[n][:, c, :],
-                    start=(c == 0),
-                    stop=(c == HALVES - 1),
-                )
-            nc.vector.tensor_copy(result[:, n, :], bank[:, 0, :])
-            if n >= EARLY_STORED - 1:
-                first = 0 if n == EARLY_STORED - 1 else n
-                nc.sync.dma_start(out=out[:, first * POINTS:(n + 1) * POINTS],
-                                  in_=result[:, first:n + 1, :].rearrange("p n v -> p (n v)"))
+            first_layer(1, 0, n, False)
+            activate(0, n)
+        cast_w1(1, 1, late[2][:], 0, 64, vcopy)
+        quantize_w1_part(1, 1, 0)
+        cast_w1(1, 1, late[3][:], 64, P, vcopy)
+        quantize_w1_part(1, 1, 1)
+        for n in range(CHUNKS):
+            first_layer(1, 1, n, False)
+            activate(1, n)
+        prepare_w2()
+        quantize_h(0, 0, CHUNKS)
+        for n in range(CHUNKS):
+            second_layer(0, n)
+        for n in range(CHUNKS):
+            quantize_h(1, n, n + 1)
+            second_layer(1, n)
+            copy_out(n, vcopy if n < 2 else scopy)
+            if n == 1:
+                store(0, 2, nc.sync)
+            elif n > 1:
+                store(n, n + 1, nc.scalar)

@@ -46,45 +46,49 @@ def tile_picked_grid_mlp_silu_sub_l_kernel(tc, xT, w1, w2, offs, out):
             for i in range(count):
                 tables[first + i] = tile[:, i, :]
 
-        def load_w1(k, a, b):
-            tile = keep.tile([P, PACK, b - a], F32, name=f"w1_raw{k}_{a}")
-            nc.sync.dma_start(out=tile[:], in_=w1_rows[k][:, :, a:b])
+        def load_w1(k, a, b, j0=0, j1=PACK):
+            tile = keep.tile([P, j1 - j0, b - a], F32, name=f"w1_raw{k}_{a}_{j0}", tag=f"w1_raw{k}_{a}_{j0}",
+                             align_bytes=64)
+            nc.sync.dma_start(out=tile[:], in_=w1_rows[k][:, j0:j1, a:b])
             return tile
 
-        w2_raw = keep.tile([P, HALVES, PACK, N], F32, name="w2_raw")
+        w2_raw = keep.tile([P, HALVES, PACK, N], F32, name="w2_raw", tag="w2_raw", align_bytes=64)
 
         def load_w2():
             nc.sync.dma_start(out=w2_raw[:], in_=w2.rearrange("(c p j) n -> p c j n", p=P, j=PACK))
 
         nc.sync.dma_start(offsets[:], offs)
-        load_tables(4, 3)
+        load_tables(0, 4)
         w1_first = load_w1(0, 0, H)
-        for level in (0, 1, 2, 3, 7):
+        load_tables(4, 2)
+        for level in (6, 7):
             load_tables(level, 1)
-        late = [load_w1(1, a, a + 256) for a in range(0, H, 256)]
+        w1_10 = load_w1(1, 0, K_PASS)
+        w1_11 = [load_w1(1, K_PASS, H, j, j + 2) for j in (0, 2)]
         load_w2()
 
         def quantize(codes, scales, grouped):
             nc.vector.quantize_mx(out=codes.bitcast(FP8X4), scales=scales, in_=grouped)
 
-        w1_grouped = [[keep.tile([P, K_PASS * PACK], BF16, name=f"w1_grouped{k}{c}", align_bytes=64)
+        w1_grouped = [[keep.tile([P, K_PASS * PACK], BF16, name=f"w1_grouped{k}{c}", tag=f"grouped{k}{c}", align_bytes=64)
                        for c in range(HALVES)] for k in range(PASSES)]
         w1_codes = [[keep.tile([P, K_PASS], U32, name=f"w1_codes{k}{c}", align_bytes=64) for c in range(HALVES)]
                     for k in range(PASSES)]
         w1_scales = [[keep.tile([P, K_PASS], U8, name=f"w1_scales{k}{c}", align_bytes=64) for c in range(HALVES)]
                      for k in range(PASSES)]
 
-        def cast_w1(k, c, raw, m0, m1, copy, ts=slice(0, PACK)):
+        def cast_w1(k, c, raw, m0, m1, copy, ts=slice(0, PACK), js=slice(0, PACK)):
             copy(
-                out=w1_grouped[k][c][:].rearrange("p (t m j) -> p m t j", t=PACK, j=PACK)[:, m0:m1, ts, :],
-                in_=raw.rearrange("p j (m t) -> p m t j", t=PACK)[:, :, ts, :],
+                out=w1_grouped[k][c][:].rearrange("p (t m j) -> p m j t", t=PACK, j=PACK)[:, m0:m1, js, ts],
+                in_=raw.rearrange("p j (m t) -> p m j t", t=PACK)[:, :, :, ts],
             )
 
         def quantize_w1(k, c, a=0, b=K_PASS):
             quantize(w1_codes[k][c][:, a:b], w1_scales[k][c][:, a:b], w1_grouped[k][c][:, PACK * a:PACK * b])
 
         x_grouped = [keep.tile([P, V, PACK], BF16, name=f"x_grouped{g}", align_bytes=64) for g in range(PASSES)]
-        x_codes = [keep.tile([P, V], U32, name=f"x_codes{g}", align_bytes=64) for g in range(PASSES)]
+        x_codes = [keep.tile([P, V], U32, name=f"x_codes{g}", tag=("w1_raw0_0_0", "x_codes1")[g], align_bytes=64)
+                   for g in range(PASSES)]
         x_scales = [keep.tile([P, V], U8, name=f"x_scales{g}", align_bytes=64) for g in range(PASSES)]
 
         def look_up(level, parts=1):
@@ -97,22 +101,32 @@ def tile_picked_grid_mlp_silu_sub_l_kernel(tc, xT, w1, w2, offs, out):
                     tables[level].indirect(offsets[:, first + v0 // 16:first + v1 // 16]),
                 )
 
+        def look_up_plain(first, count):
+            g, t = first // PACK, first % PACK
+            rows = keep.tile([P, count, V], F32, name=f"x_rows{first}")
+            for i in range(count):
+                a = (first + i) * LIST_COLS
+                nc.vector.tensor_copy(rows[:, i, :], tables[first + i].indirect(offsets[:, a:a + LIST_COLS]))
+            nc.scalar.copy(x_grouped[g][:].rearrange("p (c i) t -> p c t i", i=PACK)[:, :, t:t + count, :],
+                           rows[:].rearrange("p t (c i) -> p c t i", i=PACK))
+
         def quantize_x(g, parts=1):
             for part in range(parts):
                 v = slice(part * V // parts, (part + 1) * V // parts)
                 quantize(x_codes[g][:, v], x_scales[g][:, v], x_grouped[g][:, v, :].rearrange("p v t -> p (v t)"))
 
-        w2_grouped = keep.tile([P, HALVES, N, PACK], BF16, name="w2_grouped", align_bytes=64)
         w2_codes = keep.tile([P, HALVES, N], U32, name="w2_codes", align_bytes=64)
         w2_scales = keep.tile([P, HALVES, N], U8, name="w2_scales", align_bytes=64)
 
         def prepare_w2():
-            nc.vector.tensor_copy(w2_grouped[:], w2_raw[:].rearrange("p c j n -> p c n j"))
+            w2_grouped = keep.tile([P, HALVES, N, PACK], BF16, name="w2_grouped", tag="grouped11", align_bytes=64)
+            nc.vector.tensor_copy(w2_grouped[:].rearrange("p c (n i) j -> p c n j i", i=PACK),
+                                  w2_raw[:].rearrange("p c j (n i) -> p c n j i", i=PACK))
             quantize(w2_codes[:].rearrange("p c n -> p (c n)"), w2_scales[:].rearrange("p c n -> p (c n)"),
                      w2_grouped[:].rearrange("p c n j -> p (c n j)"))
 
         h = [keep.tile([P, V, PACK], BF16, name=f"h{c}", align_bytes=64) for c in range(HALVES)]
-        h_codes = [keep.tile([P, V], U32, name=f"h_codes{c}", align_bytes=64) for c in range(HALVES)]
+        h_codes = {}
         h_scales = [keep.tile([P, V], U8, name=f"h_scales{c}", align_bytes=64) for c in range(HALVES)]
         sums = {}
 
@@ -137,6 +151,9 @@ def tile_picked_grid_mlp_silu_sub_l_kernel(tc, xT, w1, w2, offs, out):
             nc.scalar.activation(h[c][:, v, :], sums[c, n][:].rearrange("p t v -> p v t"), SILU)
 
         def quantize_h(c, a, b):
+            if a == 0:
+                h_codes[c] = keep.tile([P, V], U32, name=f"h_codes{c}", tag="w2_raw" if c == 0 else "h_codes1",
+                                       align_bytes=64)
             v = slice(a * POINTS, b * POINTS)
             quantize(h_codes[c][:, v], h_scales[c][:, v], h[c][:, v, :].rearrange("p v t -> p (v t)"))
 
@@ -166,34 +183,34 @@ def tile_picked_grid_mlp_silu_sub_l_kernel(tc, xT, w1, w2, offs, out):
 
         vcopy, scopy = nc.vector.tensor_copy, nc.scalar.copy
 
-        def quantize_w1_part(k, c, part):
-            for t in range(PACK):
-                quantize_w1(k, c, t * P + part * 64, t * P + part * 64 + 64)
-
-        for level in (4, 5, 6):
-            look_up(level)
+        PAIRS = (slice(0, 2), slice(2, 4))
+        look_up_plain(0, 4)
         for c in range(HALVES):
-            cast_w1(0, c, w1_first[:, :, c * K_PASS:(c + 1) * K_PASS], 0, P, scopy)
+            cast_w1(0, c, w1_first[:, :, c * K_PASS:(c + 1) * K_PASS], 0, P, vcopy)
+        for c in range(HALVES):
             quantize_w1(0, c)
-        for level in (0, 1, 2, 3):
-            look_up(level)
         quantize_x(0)
         for c in range(HALVES):
             for n in range(CHUNKS):
                 first_layer(0, c, n, True)
-        look_up(7)
-        quantize_x(1)
-        cast_w1(1, 0, late[0][:], 0, 64, scopy)
-        cast_w1(1, 0, late[1][:], 64, P, vcopy)
-        quantize_w1_part(1, 0, 0)
-        quantize_w1_part(1, 0, 1)
+        look_up_plain(4, 2)
+        look_up(6)
+        look_up(7, parts=2)
+        quantize_x(1, parts=2)
+        SHARE = 40
+        for ts in PAIRS:
+            cast_w1(1, 0, w1_10[:, :, 0:4 * SHARE], 0, SHARE, scopy, ts)
+            cast_w1(1, 0, w1_10[:, :, 4 * SHARE:K_PASS], SHARE, P, vcopy, ts)
+        for a in (0, 256):
+            quantize_w1(1, 0, a, a + 256)
         for n in range(CHUNKS):
             first_layer(1, 0, n, False)
             activate(0, n)
-        cast_w1(1, 1, late[2][:], 0, 64, vcopy)
-        quantize_w1_part(1, 1, 0)
-        cast_w1(1, 1, late[3][:], 64, P, vcopy)
-        quantize_w1_part(1, 1, 1)
+        cast_w1(1, 1, w1_11[0][:], 0, P, vcopy, js=PAIRS[0])
+        for ts in PAIRS:
+            cast_w1(1, 1, w1_11[1][:], 0, P, vcopy, ts, PAIRS[1])
+        for a in (0, 256):
+            quantize_w1(1, 1, a, a + 256)
         for n in range(CHUNKS):
             first_layer(1, 1, n, False)
             activate(1, n)

@@ -63,8 +63,8 @@ def tile_picked_grid_mlp_silu_sub_l_kernel(tc, xT, w1, w2, offs, out):
         load_tables(4, 2)
         for level in (6, 7):
             load_tables(level, 1)
-        w1_10 = load_w1(1, 0, K_PASS)
-        w1_11 = [load_w1(1, K_PASS, H, j, j + 2) for j in (0, 2)]
+        w1_10 = [load_w1(1, a, a + 256) for a in (0, 256)]
+        w1_11 = [load_w1(1, a, a + 256) for a in (512, 768)]
         load_w2()
 
         def quantize(codes, scales, grouped):
@@ -197,20 +197,21 @@ def tile_picked_grid_mlp_silu_sub_l_kernel(tc, xT, w1, w2, offs, out):
         look_up(6)
         look_up(7, parts=2)
         quantize_x(1, parts=2)
-        SHARE = 40
+        SHARE = 20
+        cast_w1(1, 0, w1_10[0][:], 0, 64, scopy)
         for ts in PAIRS:
-            cast_w1(1, 0, w1_10[:, :, 0:4 * SHARE], 0, SHARE, scopy, ts)
-            cast_w1(1, 0, w1_10[:, :, 4 * SHARE:K_PASS], SHARE, P, vcopy, ts)
+            cast_w1(1, 0, w1_10[1][:, :, 0:4 * SHARE], 64, 64 + SHARE, scopy, ts)
+            cast_w1(1, 0, w1_10[1][:, :, 4 * SHARE:256], 64 + SHARE, P, vcopy, ts)
         for a in (0, 256):
             quantize_w1(1, 0, a, a + 256)
         for n in range(CHUNKS):
             first_layer(1, 0, n, False)
             activate(0, n)
-        cast_w1(1, 1, w1_11[0][:], 0, P, vcopy, js=PAIRS[0])
-        for ts in PAIRS:
-            cast_w1(1, 1, w1_11[1][:], 0, P, vcopy, ts, PAIRS[1])
-        for a in (0, 256):
-            quantize_w1(1, 1, a, a + 256)
+        for part in range(2):
+            for ts in PAIRS:
+                cast_w1(1, 1, w1_11[part][:], 64 * part, 64 * part + 64, vcopy, ts)
+            for t in range(PACK):
+                quantize_w1(1, 1, t * P + part * 64, t * P + part * 64 + 64)
         for n in range(CHUNKS):
             first_layer(1, 1, n, False)
             activate(1, n)

@@ -27,7 +27,8 @@ def tile_picked_grid_mlp_silu_sub_l_kernel(tc, xT, w1, w2, offs, out):
     nc = tc.nc
     with ExitStack() as ctx:
         keep = ctx.enter_context(tc.tile_pool(name="keep", bufs=1))
-        banks = ctx.enter_context(tc.psum_pool(name="banks", bufs=8))
+        banks = ctx.enter_context(tc.psum_pool(name="banks", bufs=6))
+        out_banks = ctx.enter_context(tc.psum_pool(name="out_banks", bufs=2))
 
         table_loader = keep.tile([P, 2], F32, name="table_loader")
         nc.vector.memset(table_loader[:], 0.0)
@@ -41,7 +42,7 @@ def tile_picked_grid_mlp_silu_sub_l_kernel(tc, xT, w1, w2, offs, out):
 
         def load_tables(first, count):
             g, t = first // PACK, first % PACK
-            tile = keep.tile([P, count, T], F32, name=f"tables{first}")
+            tile = keep.tile([P, count, T], F32, name=f"tables{first}", tag=f"tables{first}", align_bytes=64)
             nc.sync.dma_start(out=tile[:], in_=xT_rows[g][:, t:t + count, :])
             for i in range(count):
                 tables[first + i] = tile[:, i, :]
@@ -59,10 +60,11 @@ def tile_picked_grid_mlp_silu_sub_l_kernel(tc, xT, w1, w2, offs, out):
 
         nc.sync.dma_start(offsets[:], offs)
         load_tables(0, 4)
-        w1_first = load_w1(0, 0, H)
+        w1_first = load_w1(0, 0, 768)
         load_tables(4, 2)
         for level in (6, 7):
             load_tables(level, 1)
+        w1_01 = load_w1(0, 768, H)
         w1_10 = [load_w1(1, a, a + 256) for a in (0, 256)]
         w1_11 = [load_w1(1, a, a + 256) for a in (512, 768)]
         load_w2()
@@ -87,7 +89,7 @@ def tile_picked_grid_mlp_silu_sub_l_kernel(tc, xT, w1, w2, offs, out):
             quantize(w1_codes[k][c][:, a:b], w1_scales[k][c][:, a:b], w1_grouped[k][c][:, PACK * a:PACK * b])
 
         x_grouped = [keep.tile([P, V, PACK], BF16, name=f"x_grouped{g}", align_bytes=64) for g in range(PASSES)]
-        x_codes = [keep.tile([P, V], U32, name=f"x_codes{g}", tag=("w1_raw0_0_0", "x_codes1")[g], align_bytes=64)
+        x_codes = [keep.tile([P, V], U32, name=f"x_codes{g}", tag=("tables6", "x_codes1")[g], align_bytes=64)
                    for g in range(PASSES)]
         x_scales = [keep.tile([P, V], U8, name=f"x_scales{g}", align_bytes=64) for g in range(PASSES)]
 
@@ -162,7 +164,7 @@ def tile_picked_grid_mlp_silu_sub_l_kernel(tc, xT, w1, w2, offs, out):
         def second_layer(c, n):
             v = slice(n * POINTS, (n + 1) * POINTS)
             if c == 0:
-                outs[n] = banks.tile([P, PACK, POINTS], F32, name="out_bank", tag="bank")
+                outs[n] = out_banks.tile([P, PACK, POINTS], F32, name="out_bank")
             nc.tensor.matmul_mx(
                 out=outs[n][:, 0, :],
                 lhsT=w2_codes[:, c, :].bitcast(FP8X4),
@@ -184,29 +186,38 @@ def tile_picked_grid_mlp_silu_sub_l_kernel(tc, xT, w1, w2, offs, out):
         vcopy, scopy = nc.vector.tensor_copy, nc.scalar.copy
 
         PAIRS = (slice(0, 2), slice(2, 4))
+
+        def quantize_w1_part(k, c, part):
+            for t in range(PACK):
+                quantize_w1(k, c, t * P + part * 64, t * P + part * 64 + 64)
+
         look_up_plain(0, 4)
-        for c in range(HALVES):
-            cast_w1(0, c, w1_first[:, :, c * K_PASS:(c + 1) * K_PASS], 0, P, vcopy)
-        for c in range(HALVES):
-            quantize_w1(0, c)
-        quantize_x(0)
-        for c in range(HALVES):
-            for n in range(CHUNKS):
-                first_layer(0, c, n, True)
+        cast_w1(0, 0, w1_first[:, :, 0:K_PASS], 0, P, vcopy)
+        cast_w1(0, 1, w1_first[:, :, K_PASS:768], 0, 64, vcopy)
+        quantize_w1(0, 0)
+        quantize_w1_part(0, 1, 0)
         look_up_plain(4, 2)
         look_up(6)
+        quantize_x(0)
+        for n in range(CHUNKS):
+            first_layer(0, 0, n, True)
         look_up(7, parts=2)
         quantize_x(1, parts=2)
-        SHARE = 20
-        cast_w1(1, 0, w1_10[0][:], 0, 64, scopy)
+        cast_w1(0, 1, w1_01[:], 64, P, scopy)
+        quantize_w1_part(0, 1, 1)
+        cast_w1(1, 0, w1_10[0][:, :, 0:128], 0, 32, scopy)
+        cast_w1(1, 0, w1_10[0][:, :, 128:256], 32, 64, vcopy)
+        quantize_w1_part(1, 0, 0)
+        SHARE = 24
         for ts in PAIRS:
             cast_w1(1, 0, w1_10[1][:, :, 0:4 * SHARE], 64, 64 + SHARE, scopy, ts)
             cast_w1(1, 0, w1_10[1][:, :, 4 * SHARE:256], 64 + SHARE, P, vcopy, ts)
-        for a in (0, 256):
-            quantize_w1(1, 0, a, a + 256)
+        quantize_w1_part(1, 0, 1)
         for n in range(CHUNKS):
             first_layer(1, 0, n, False)
             activate(0, n)
+        for n in range(CHUNKS):
+            first_layer(0, 1, n, True)
         for part in range(2):
             for ts in PAIRS:
                 cast_w1(1, 1, w1_11[part][:], 64 * part, 64 * part + 64, vcopy, ts)
@@ -219,7 +230,6 @@ def tile_picked_grid_mlp_silu_sub_l_kernel(tc, xT, w1, w2, offs, out):
         quantize_h(0, 0, CHUNKS)
         for n in range(CHUNKS):
             second_layer(0, n)
-        for n in range(CHUNKS):
             quantize_h(1, n, n + 1)
             second_layer(1, n)
             copy_out(n, vcopy if n < 2 else scopy)

@@ -21,219 +21,209 @@ HALVES = H // K_PASS
 POINTS = 128
 CHUNKS = V // POINTS
 LIST_COLS = V // 16
+PIECE = K_PASS // 2
+PIECE_ROWS = PIECE // PACK
+SCALAR_ROWS = 24
+ALL_TILES = slice(0, PACK)
+TILE_PAIRS = (slice(0, 2), slice(2, 4))
+OUT_BANKS = 2
 
 
 def tile_picked_grid_mlp_silu_sub_l_kernel(tc, xT, w1, w2, offs, out):
     nc = tc.nc
+    on_vector, on_scalar = nc.vector.tensor_copy, nc.scalar.copy
     with ExitStack() as ctx:
         keep = ctx.enter_context(tc.tile_pool(name="keep", bufs=1))
-        banks = ctx.enter_context(tc.psum_pool(name="banks", bufs=6))
-        out_banks = ctx.enter_context(tc.psum_pool(name="out_banks", bufs=2))
+        banks = ctx.enter_context(tc.psum_pool(name="banks", bufs=8 - OUT_BANKS))
+        out_banks = ctx.enter_context(tc.psum_pool(name="out_banks", bufs=OUT_BANKS))
 
         table_loader = keep.tile([P, 2], F32, name="table_loader")
         nc.vector.memset(table_loader[:], 0.0)
         nc.scalar.activation(table_loader[:, 1:2], table_loader[:, 0:1], SILU)
 
-        w1_rows = [w1[k * K_PASS:(k + 1) * K_PASS, :].rearrange("(p j) w -> p j w", j=PACK) for k in range(PASSES)]
-        xT_rows = [xT[g * K_PASS:(g + 1) * K_PASS, :].rearrange("(f j) w -> f j w", j=PACK) for g in range(PASSES)]
-
-        offsets = keep.tile([P, LEVELS * LIST_COLS], U16, name="offsets")
+        w1_rows = [w1[g * K_PASS:(g + 1) * K_PASS, :].rearrange("(p j) w -> p j w", j=PACK) for g in range(PASSES)]
+        xT_rows = [xT[g * K_PASS:(g + 1) * K_PASS, :].rearrange("(p t) w -> p t w", t=PACK) for g in range(PASSES)]
         tables = {}
 
         def load_tables(first, count):
-            g, t = first // PACK, first % PACK
+            g, t = divmod(first, PACK)
             tile = keep.tile([P, count, T], F32, name=f"tables{first}", tag=f"tables{first}", align_bytes=64)
             nc.sync.dma_start(out=tile[:], in_=xT_rows[g][:, t:t + count, :])
             for i in range(count):
                 tables[first + i] = tile[:, i, :]
 
-        def load_w1(k, a, b, j0=0, j1=PACK):
-            tile = keep.tile([P, j1 - j0, b - a], F32, name=f"w1_raw{k}_{a}_{j0}", tag=f"w1_raw{k}_{a}_{j0}",
-                             align_bytes=64)
-            nc.sync.dma_start(out=tile[:], in_=w1_rows[k][:, j0:j1, a:b])
+        def load_w1(g, a, b):
+            tile = keep.tile([P, PACK, b - a], F32, name=f"w1_raw{g}_{a}", align_bytes=64)
+            nc.sync.dma_start(out=tile[:], in_=w1_rows[g][:, :, a:b])
             return tile
 
+        offsets = keep.tile([P, LEVELS * LIST_COLS], U16, name="offsets")
         w2_raw = keep.tile([P, HALVES, PACK, N], F32, name="w2_raw", tag="w2_raw", align_bytes=64)
-
-        def load_w2():
-            nc.sync.dma_start(out=w2_raw[:], in_=w2.rearrange("(c p j) n -> p c j n", p=P, j=PACK))
-
         nc.sync.dma_start(offsets[:], offs)
         load_tables(0, 4)
-        w1_first = load_w1(0, 0, 768)
+        w1_early = load_w1(0, 0, H - PIECE)
         load_tables(4, 2)
-        for level in (6, 7):
-            load_tables(level, 1)
-        w1_01 = load_w1(0, 768, H)
-        w1_10 = [load_w1(1, a, a + 256) for a in (0, 256)]
-        w1_11 = [load_w1(1, a, a + 256) for a in (512, 768)]
-        load_w2()
+        load_tables(6, 1)
+        load_tables(7, 1)
+        w1_rest = load_w1(0, H - PIECE, H)
+        w1_late = [[load_w1(1, c * K_PASS + a, c * K_PASS + a + PIECE) for a in (0, PIECE)] for c in range(HALVES)]
+        nc.sync.dma_start(out=w2_raw[:], in_=w2.rearrange("(c p j) n -> p c j n", p=P, j=PACK))
 
-        def quantize(codes, scales, grouped):
-            nc.vector.quantize_mx(out=codes.bitcast(FP8X4), scales=scales, in_=grouped)
+        def quantize(codes, scales, interleaved):
+            nc.vector.quantize_mx(out=codes.bitcast(FP8X4), scales=scales, in_=interleaved)
 
-        w1_grouped = [[keep.tile([P, K_PASS * PACK], BF16, name=f"w1_grouped{k}{c}", tag=f"grouped{k}{c}", align_bytes=64)
-                       for c in range(HALVES)] for k in range(PASSES)]
-        w1_codes = [[keep.tile([P, K_PASS], U32, name=f"w1_codes{k}{c}", align_bytes=64) for c in range(HALVES)]
-                    for k in range(PASSES)]
-        w1_scales = [[keep.tile([P, K_PASS], U8, name=f"w1_scales{k}{c}", align_bytes=64) for c in range(HALVES)]
-                     for k in range(PASSES)]
+        def w1_tiles(kind, width, dtype):
+            return [[keep.tile([P, width], dtype, name=f"w1_{kind}{g}{c}", tag=f"w1_{kind}{g}{c}", align_bytes=64)
+                     for c in range(HALVES)] for g in range(PASSES)]
 
-        def cast_w1(k, c, raw, m0, m1, copy, ts=slice(0, PACK), js=slice(0, PACK)):
+        w1_bf16 = w1_tiles("bf16_", K_PASS * PACK, BF16)
+        w1_codes = w1_tiles("codes", K_PASS, U32)
+        w1_scales = w1_tiles("scales", K_PASS, U8)
+
+        def cast_w1(g, c, raw, m0, m1, copy, tiles=ALL_TILES):
             copy(
-                out=w1_grouped[k][c][:].rearrange("p (t m j) -> p m j t", t=PACK, j=PACK)[:, m0:m1, js, ts],
-                in_=raw.rearrange("p j (m t) -> p m j t", t=PACK)[:, :, :, ts],
+                out=w1_bf16[g][c][:].rearrange("p (t m j) -> p m j t", t=PACK, j=PACK)[:, m0:m1, :, tiles],
+                in_=raw.rearrange("p j (m t) -> p m j t", t=PACK)[:, :, :, tiles],
             )
 
-        def quantize_w1(k, c, a=0, b=K_PASS):
-            quantize(w1_codes[k][c][:, a:b], w1_scales[k][c][:, a:b], w1_grouped[k][c][:, PACK * a:PACK * b])
+        def cast_w1_shared(g, c, piece, raw, tiles=ALL_TILES):
+            m0 = piece * PIECE_ROWS
+            cast_w1(g, c, raw[:, :, 0:PACK * SCALAR_ROWS], m0, m0 + SCALAR_ROWS, on_scalar, tiles)
+            cast_w1(g, c, raw[:, :, PACK * SCALAR_ROWS:PIECE], m0 + SCALAR_ROWS, m0 + PIECE_ROWS, on_vector, tiles)
 
-        x_grouped = [keep.tile([P, V, PACK], BF16, name=f"x_grouped{g}", align_bytes=64) for g in range(PASSES)]
-        x_codes = [keep.tile([P, V], U32, name=f"x_codes{g}", tag=("tables6", "x_codes1")[g], align_bytes=64)
-                   for g in range(PASSES)]
+        def quantize_w1(g, c, a, b):
+            quantize(w1_codes[g][c][:, a:b], w1_scales[g][c][:, a:b], w1_bf16[g][c][:, PACK * a:PACK * b])
+
+        def quantize_w1_piece(g, c, piece):
+            for t in range(PACK):
+                a = t * P + piece * PIECE_ROWS
+                quantize_w1(g, c, a, a + PIECE_ROWS)
+
+        x_bf16 = [keep.tile([P, V, PACK], BF16, name=f"x_bf16_{g}", align_bytes=64) for g in range(PASSES)]
+        x_codes = [keep.tile([P, V], U32, name=f"x_codes{g}", tag=tag, align_bytes=64)
+                   for g, tag in enumerate(("tables6", "x_codes1"))]
         x_scales = [keep.tile([P, V], U8, name=f"x_scales{g}", align_bytes=64) for g in range(PASSES)]
 
+        def entries(level, v0, v1):
+            return tables[level].indirect(offsets[:, level * LIST_COLS + v0 // 16:level * LIST_COLS + v1 // 16])
+
         def look_up(level, parts=1):
-            g, t = level // PACK, level % PACK
+            g, t = divmod(level, PACK)
             for part in range(parts):
                 v0, v1 = part * V // parts, (part + 1) * V // parts
-                first = level * LIST_COLS
-                nc.vector.tensor_copy(
-                    x_grouped[g][:, v0:v1, t],
-                    tables[level].indirect(offsets[:, first + v0 // 16:first + v1 // 16]),
-                )
+                nc.vector.tensor_copy(x_bf16[g][:, v0:v1, t], entries(level, v0, v1))
 
-        def look_up_plain(first, count):
-            g, t = first // PACK, first % PACK
+        def look_up_rows(first, count):
+            g, t = divmod(first, PACK)
             rows = keep.tile([P, count, V], F32, name=f"x_rows{first}")
             for i in range(count):
-                a = (first + i) * LIST_COLS
-                nc.vector.tensor_copy(rows[:, i, :], tables[first + i].indirect(offsets[:, a:a + LIST_COLS]))
-            nc.scalar.copy(x_grouped[g][:].rearrange("p (c i) t -> p c t i", i=PACK)[:, :, t:t + count, :],
-                           rows[:].rearrange("p t (c i) -> p c t i", i=PACK))
+                nc.vector.tensor_copy(rows[:, i, :], entries(first + i, 0, V))
+            nc.scalar.copy(x_bf16[g][:].rearrange("p (u i) t -> p u t i", i=PACK)[:, :, t:t + count, :],
+                           rows[:].rearrange("p t (u i) -> p u t i", i=PACK))
 
         def quantize_x(g, parts=1):
             for part in range(parts):
                 v = slice(part * V // parts, (part + 1) * V // parts)
-                quantize(x_codes[g][:, v], x_scales[g][:, v], x_grouped[g][:, v, :].rearrange("p v t -> p (v t)"))
+                quantize(x_codes[g][:, v], x_scales[g][:, v], x_bf16[g][:, v, :].rearrange("p v t -> p (v t)"))
 
         w2_codes = keep.tile([P, HALVES, N], U32, name="w2_codes", align_bytes=64)
         w2_scales = keep.tile([P, HALVES, N], U8, name="w2_scales", align_bytes=64)
 
         def prepare_w2():
-            w2_grouped = keep.tile([P, HALVES, N, PACK], BF16, name="w2_grouped", tag="grouped11", align_bytes=64)
-            nc.vector.tensor_copy(w2_grouped[:].rearrange("p c (n i) j -> p c n j i", i=PACK),
-                                  w2_raw[:].rearrange("p c j (n i) -> p c n j i", i=PACK))
+            w2_bf16 = keep.tile([P, HALVES, N, PACK], BF16, name="w2_bf16", tag="w1_bf16_11", align_bytes=64)
+            nc.vector.tensor_copy(w2_bf16[:].rearrange("p c (u i) j -> p c u j i", i=PACK),
+                                  w2_raw[:].rearrange("p c j (u i) -> p c u j i", i=PACK))
             quantize(w2_codes[:].rearrange("p c n -> p (c n)"), w2_scales[:].rearrange("p c n -> p (c n)"),
-                     w2_grouped[:].rearrange("p c n j -> p (c n j)"))
+                     w2_bf16[:].rearrange("p c n j -> p (c n j)"))
 
-        h = [keep.tile([P, V, PACK], BF16, name=f"h{c}", align_bytes=64) for c in range(HALVES)]
-        h_codes = {}
+        h_bf16 = [keep.tile([P, V, PACK], BF16, name=f"h_bf16_{c}", align_bytes=64) for c in range(HALVES)]
         h_scales = [keep.tile([P, V], U8, name=f"h_scales{c}", align_bytes=64) for c in range(HALVES)]
         sums = {}
 
-        def first_layer(k, c, n, first):
-            v = slice(n * POINTS, (n + 1) * POINTS)
-            if first:
-                sums[c, n] = banks.tile([P, PACK, POINTS], F32, name="bank", tag="bank")
+        def points(first, count=1):
+            return slice(first * POINTS, (first + count) * POINTS)
+
+        def first_layer(g, c, n):
+            if g == 0:
+                sums[c, n] = banks.tile([P, PACK, POINTS], F32, name="bank")
             for t in range(PACK):
                 channels = slice(t * P, (t + 1) * P)
                 nc.tensor.matmul_mx(
                     out=sums[c, n][:, t, :],
-                    lhsT=w1_codes[k][c][:, channels].bitcast(FP8X4),
-                    lhsT_scale=w1_scales[k][c][:, channels],
-                    rhs=x_codes[k][:, v].bitcast(FP8X4),
-                    rhs_scale=x_scales[k][:, v],
-                    start=(first and t == 0),
-                    stop=(not first and t == PACK - 1),
+                    lhsT=w1_codes[g][c][:, channels].bitcast(FP8X4),
+                    lhsT_scale=w1_scales[g][c][:, channels],
+                    rhs=x_codes[g][:, points(n)].bitcast(FP8X4),
+                    rhs_scale=x_scales[g][:, points(n)],
+                    start=(g == 0 and t == 0),
+                    stop=(g == PASSES - 1 and t == PACK - 1),
                 )
 
         def activate(c, n):
-            v = slice(n * POINTS, (n + 1) * POINTS)
-            nc.scalar.activation(h[c][:, v, :], sums[c, n][:].rearrange("p t v -> p v t"), SILU)
+            nc.scalar.activation(h_bf16[c][:, points(n), :], sums[c, n][:].rearrange("p t v -> p v t"), SILU)
 
-        def quantize_h(c, a, b):
-            if a == 0:
-                h_codes[c] = keep.tile([P, V], U32, name=f"h_codes{c}", tag="w2_raw" if c == 0 else "h_codes1",
-                                       align_bytes=64)
-            v = slice(a * POINTS, b * POINTS)
-            quantize(h_codes[c][:, v], h_scales[c][:, v], h[c][:, v, :].rearrange("p v t -> p (v t)"))
+        def quantize_h(c, codes, v):
+            quantize(codes[:, v], h_scales[c][:, v], h_bf16[c][:, v, :].rearrange("p v t -> p (v t)"))
 
-        outs = {}
-
-        def second_layer(c, n):
-            v = slice(n * POINTS, (n + 1) * POINTS)
-            if c == 0:
-                outs[n] = out_banks.tile([P, PACK, POINTS], F32, name="out_bank")
+        def second_layer(c, n, codes, bank):
             nc.tensor.matmul_mx(
-                out=outs[n][:, 0, :],
+                out=bank[:, 0:POINTS],
                 lhsT=w2_codes[:, c, :].bitcast(FP8X4),
                 lhsT_scale=w2_scales[:, c, :],
-                rhs=h_codes[c][:, v].bitcast(FP8X4),
-                rhs_scale=h_scales[c][:, v],
+                rhs=codes[:, points(n)].bitcast(FP8X4),
+                rhs_scale=h_scales[c][:, points(n)],
                 start=(c == 0),
                 stop=(c == HALVES - 1),
             )
 
         result = keep.tile([P, V], F32, name="result", align_bytes=64)
 
-        def copy_out(n, copy):
-            copy(result[:, n * POINTS:(n + 1) * POINTS], outs[n][:, 0, :])
+        look_up_rows(0, 4)
+        cast_w1(0, 0, w1_early[:, :, 0:K_PASS], 0, P, on_vector)
+        cast_w1(0, 1, w1_early[:, :, K_PASS:H - PIECE], 0, PIECE_ROWS, on_vector)
+        quantize_w1(0, 0, 0, K_PASS)
+        quantize_w1_piece(0, 1, 0)
 
-        def store(a, b, queue):
-            queue.dma_start(out=out[:, a * POINTS:b * POINTS], in_=result[:, a * POINTS:b * POINTS])
-
-        vcopy, scopy = nc.vector.tensor_copy, nc.scalar.copy
-
-        PAIRS = (slice(0, 2), slice(2, 4))
-
-        def quantize_w1_part(k, c, part):
-            for t in range(PACK):
-                quantize_w1(k, c, t * P + part * 64, t * P + part * 64 + 64)
-
-        look_up_plain(0, 4)
-        cast_w1(0, 0, w1_first[:, :, 0:K_PASS], 0, P, vcopy)
-        cast_w1(0, 1, w1_first[:, :, K_PASS:768], 0, 64, vcopy)
-        quantize_w1(0, 0)
-        quantize_w1_part(0, 1, 0)
-        look_up_plain(4, 2)
+        look_up_rows(4, 2)
         look_up(6)
         quantize_x(0)
         for n in range(CHUNKS):
-            first_layer(0, 0, n, True)
+            first_layer(0, 0, n)
         look_up(7, parts=2)
         quantize_x(1, parts=2)
-        cast_w1(0, 1, w1_01[:], 64, P, scopy)
-        quantize_w1_part(0, 1, 1)
-        cast_w1(1, 0, w1_10[0][:, :, 0:128], 0, 32, scopy)
-        cast_w1(1, 0, w1_10[0][:, :, 128:256], 32, 64, vcopy)
-        quantize_w1_part(1, 0, 0)
-        SHARE = 24
-        for ts in PAIRS:
-            cast_w1(1, 0, w1_10[1][:, :, 0:4 * SHARE], 64, 64 + SHARE, scopy, ts)
-            cast_w1(1, 0, w1_10[1][:, :, 4 * SHARE:256], 64 + SHARE, P, vcopy, ts)
-        quantize_w1_part(1, 0, 1)
+        cast_w1(0, 1, w1_rest[:], PIECE_ROWS, P, on_scalar)
+        quantize_w1_piece(0, 1, 1)
+
+        cast_w1_shared(1, 0, 0, w1_late[0][0])
+        quantize_w1_piece(1, 0, 0)
+        for tiles in TILE_PAIRS:
+            cast_w1_shared(1, 0, 1, w1_late[0][1], tiles)
+        quantize_w1_piece(1, 0, 1)
         for n in range(CHUNKS):
-            first_layer(1, 0, n, False)
+            first_layer(1, 0, n)
             activate(0, n)
+
         for n in range(CHUNKS):
-            first_layer(0, 1, n, True)
-        for part in range(2):
-            for ts in PAIRS:
-                cast_w1(1, 1, w1_11[part][:], 64 * part, 64 * part + 64, vcopy, ts)
-            for t in range(PACK):
-                quantize_w1(1, 1, t * P + part * 64, t * P + part * 64 + 64)
+            first_layer(0, 1, n)
+        for piece in range(2):
+            for tiles in TILE_PAIRS:
+                cast_w1(1, 1, w1_late[1][piece][:], piece * PIECE_ROWS, (piece + 1) * PIECE_ROWS, on_vector, tiles)
+            quantize_w1_piece(1, 1, piece)
         for n in range(CHUNKS):
-            first_layer(1, 1, n, False)
+            first_layer(1, 1, n)
             activate(1, n)
+
         prepare_w2()
-        quantize_h(0, 0, CHUNKS)
+        h_codes0 = keep.tile([P, V], U32, name="h_codes0", tag="w2_raw", align_bytes=64)
+        quantize_h(0, h_codes0, points(0, CHUNKS))
+        h_codes1 = keep.tile([P, V], U32, name="h_codes1", align_bytes=64)
         for n in range(CHUNKS):
-            second_layer(0, n)
-            quantize_h(1, n, n + 1)
-            second_layer(1, n)
-            copy_out(n, vcopy if n < 2 else scopy)
+            bank = out_banks.tile([P, V], F32, name="out_bank")
+            second_layer(0, n, h_codes0, bank)
+            quantize_h(1, h_codes1, points(n))
+            second_layer(1, n, h_codes1, bank)
+            copy = on_vector if n == 0 else on_scalar
+            copy(result[:, points(n)], bank[:, 0:POINTS])
             if n == 1:
-                store(0, 2, nc.sync)
+                nc.sync.dma_start(out=out[:, points(0, 2)], in_=result[:, points(0, 2)])
             elif n > 1:
-                store(n, n + 1, nc.scalar)
+                nc.scalar.dma_start(out=out[:, points(n)], in_=result[:, points(n)])

@@ -37,10 +37,6 @@ def tile_picked_grid_mlp_silu_sub_l_kernel(tc, xT, w1, w2, offs, out):
         banks = ctx.enter_context(tc.psum_pool(name="banks", bufs=8 - OUT_BANKS))
         out_banks = ctx.enter_context(tc.psum_pool(name="out_banks", bufs=OUT_BANKS))
 
-        table_loader = keep.tile([P, 2], F32, name="table_loader")
-        nc.vector.memset(table_loader[:], 0.0)
-        nc.scalar.activation(table_loader[:, 1:2], table_loader[:, 0:1], SILU)
-
         w1_rows = [w1[g * K_PASS:(g + 1) * K_PASS, :].rearrange("(p j) w -> p j w", j=PACK) for g in range(PASSES)]
         xT_rows = [xT[g * K_PASS:(g + 1) * K_PASS, :].rearrange("(p t) w -> p t w", t=PACK) for g in range(PASSES)]
         tables = {}
@@ -53,7 +49,7 @@ def tile_picked_grid_mlp_silu_sub_l_kernel(tc, xT, w1, w2, offs, out):
                 tables[first + i] = tile[:, i, :]
 
         def load_w1(g, a, b):
-            tile = keep.tile([P, PACK, b - a], F32, name=f"w1_raw{g}_{a}", align_bytes=64)
+            tile = keep.tile([P, PACK, b - a], F32, name=f"w1_raw{g}_{a}", tag=f"w1_raw{g}_{a}", align_bytes=64)
             nc.sync.dma_start(out=tile[:], in_=w1_rows[g][:, :, a:b])
             return tile
 
@@ -62,9 +58,8 @@ def tile_picked_grid_mlp_silu_sub_l_kernel(tc, xT, w1, w2, offs, out):
         nc.sync.dma_start(offsets[:], offs)
         load_tables(0, 4)
         w1_early = load_w1(0, 0, H - PIECE)
-        load_tables(4, 2)
-        load_tables(6, 1)
-        load_tables(7, 1)
+        for level in (4, 5, 6, 7):
+            load_tables(level, 1)
         w1_rest = load_w1(0, H - PIECE, H)
         w1_late = [[load_w1(1, c * K_PASS + a, c * K_PASS + a + PIECE) for a in (0, PIECE)] for c in range(HALVES)]
         nc.sync.dma_start(out=w2_raw[:], in_=w2.rearrange("(c p j) n -> p c j n", p=P, j=PACK))
@@ -86,11 +81,6 @@ def tile_picked_grid_mlp_silu_sub_l_kernel(tc, xT, w1, w2, offs, out):
                 in_=raw.rearrange("p j (m t) -> p m j t", t=PACK)[:, :, :, tiles],
             )
 
-        def cast_w1_shared(g, c, piece, raw, tiles=ALL_TILES):
-            m0 = piece * PIECE_ROWS
-            cast_w1(g, c, raw[:, :, 0:PACK * SCALAR_ROWS], m0, m0 + SCALAR_ROWS, on_scalar, tiles)
-            cast_w1(g, c, raw[:, :, PACK * SCALAR_ROWS:PIECE], m0 + SCALAR_ROWS, m0 + PIECE_ROWS, on_vector, tiles)
-
         def quantize_w1(g, c, a, b):
             quantize(w1_codes[g][c][:, a:b], w1_scales[g][c][:, a:b], w1_bf16[g][c][:, PACK * a:PACK * b])
 
@@ -99,7 +89,8 @@ def tile_picked_grid_mlp_silu_sub_l_kernel(tc, xT, w1, w2, offs, out):
                 a = t * P + piece * PIECE_ROWS
                 quantize_w1(g, c, a, a + PIECE_ROWS)
 
-        x_bf16 = [keep.tile([P, V, PACK], BF16, name=f"x_bf16_{g}", align_bytes=64) for g in range(PASSES)]
+        x_bf16 = [keep.tile([P, V, PACK], BF16, name=f"x_bf16_{g}", tag=tag, align_bytes=64)
+                  for g, tag in enumerate(("w1_raw0_0", "x_bf16_1"))]
         x_codes = [keep.tile([P, V], U32, name=f"x_codes{g}", tag=tag, align_bytes=64)
                    for g, tag in enumerate(("tables6", "x_codes1"))]
         x_scales = [keep.tile([P, V], U8, name=f"x_scales{g}", align_bytes=64) for g in range(PASSES)]
@@ -177,9 +168,9 @@ def tile_picked_grid_mlp_silu_sub_l_kernel(tc, xT, w1, w2, offs, out):
 
         result = keep.tile([P, V], F32, name="result", align_bytes=64)
 
+        cast_w1(0, 0, w1_early[:, :, 0:K_PASS], 0, P, on_scalar)
+        cast_w1(0, 1, w1_early[:, :, K_PASS:H - PIECE], 0, PIECE_ROWS, on_scalar)
         look_up_rows(0, 4)
-        cast_w1(0, 0, w1_early[:, :, 0:K_PASS], 0, P, on_vector)
-        cast_w1(0, 1, w1_early[:, :, K_PASS:H - PIECE], 0, PIECE_ROWS, on_vector)
         quantize_w1(0, 0, 0, K_PASS)
         quantize_w1_piece(0, 1, 0)
 
@@ -193,10 +184,11 @@ def tile_picked_grid_mlp_silu_sub_l_kernel(tc, xT, w1, w2, offs, out):
         cast_w1(0, 1, w1_rest[:], PIECE_ROWS, P, on_scalar)
         quantize_w1_piece(0, 1, 1)
 
-        cast_w1_shared(1, 0, 0, w1_late[0][0])
+        cast_w1(1, 0, w1_late[0][0][:, :, 0:PACK * SCALAR_ROWS], 0, SCALAR_ROWS, on_scalar)
+        cast_w1(1, 0, w1_late[0][0][:, :, PACK * SCALAR_ROWS:PIECE], SCALAR_ROWS, PIECE_ROWS, on_vector)
         quantize_w1_piece(1, 0, 0)
         for tiles in TILE_PAIRS:
-            cast_w1_shared(1, 0, 1, w1_late[0][1], tiles)
+            cast_w1(1, 0, w1_late[0][1][:], PIECE_ROWS, P, on_vector, tiles)
         quantize_w1_piece(1, 0, 1)
         for n in range(CHUNKS):
             first_layer(1, 0, n)

@@ -12,6 +12,7 @@ U16 = mybir.dt.uint16
 U8 = mybir.dt.uint8
 FP8X4 = mybir.dt.float8_e4m3fn_x4
 SILU = mybir.ActivationFunctionType.Silu
+COPY = mybir.ActivationFunctionType.Copy
 
 P = 128
 PACK = 4
@@ -23,7 +24,6 @@ CHUNKS = V // POINTS
 LIST_COLS = V // 16
 PIECE = K_PASS // 2
 PIECE_ROWS = PIECE // PACK
-SCALAR_ROWS = 24
 ALL_TILES = slice(0, PACK)
 TILE_PAIRS = (slice(0, 2), slice(2, 4))
 OUT_BANKS = 2
@@ -36,6 +36,10 @@ def tile_picked_grid_mlp_silu_sub_l_kernel(tc, xT, w1, w2, offs, out):
         keep = ctx.enter_context(tc.tile_pool(name="keep", bufs=1))
         banks = ctx.enter_context(tc.psum_pool(name="banks", bufs=8 - OUT_BANKS))
         out_banks = ctx.enter_context(tc.psum_pool(name="out_banks", bufs=OUT_BANKS))
+
+        warm = keep.tile([P, 2], F32, name="warm")
+        nc.gpsimd.memset(warm[:, 0:1], 0.0)
+        nc.scalar.activation(warm[:, 1:2], warm[:, 0:1], SILU)
 
         w1_rows = [w1[g * K_PASS:(g + 1) * K_PASS, :].rearrange("(p j) w -> p j w", j=PACK) for g in range(PASSES)]
         xT_rows = [xT[g * K_PASS:(g + 1) * K_PASS, :].rearrange("(p t) w -> p t w", t=PACK) for g in range(PASSES)]
@@ -57,11 +61,13 @@ def tile_picked_grid_mlp_silu_sub_l_kernel(tc, xT, w1, w2, offs, out):
         w2_raw = keep.tile([P, HALVES, PACK, N], F32, name="w2_raw", tag="w2_raw", align_bytes=64)
         nc.sync.dma_start(offsets[:], offs)
         load_tables(0, 4)
-        w1_early = load_w1(0, 0, H - PIECE)
-        for level in (4, 5, 6, 7):
+        w1_early = load_w1(0, 0, K_PASS)
+        load_tables(4, 2)
+        for level in (6, 7):
             load_tables(level, 1)
-        w1_rest = load_w1(0, H - PIECE, H)
-        w1_late = [[load_w1(1, c * K_PASS + a, c * K_PASS + a + PIECE) for a in (0, PIECE)] for c in range(HALVES)]
+        w1_late = [[load_w1(1, a, a + PIECE) for a in (0, PIECE)]]
+        w1_rest = [load_w1(0, K_PASS + a, K_PASS + a + PIECE) for a in (0, PIECE)]
+        w1_late.append([load_w1(1, K_PASS + a, K_PASS + a + PIECE) for a in (0, PIECE)])
         nc.sync.dma_start(out=w2_raw[:], in_=w2.rearrange("(c p j) n -> p c j n", p=P, j=PACK))
 
         def quantize(codes, scales, interleaved):
@@ -90,7 +96,7 @@ def tile_picked_grid_mlp_silu_sub_l_kernel(tc, xT, w1, w2, offs, out):
                 quantize_w1(g, c, a, a + PIECE_ROWS)
 
         x_bf16 = [keep.tile([P, V, PACK], BF16, name=f"x_bf16_{g}", tag=tag, align_bytes=64)
-                  for g, tag in enumerate(("w1_raw0_0", "x_bf16_1"))]
+                  for g, tag in enumerate(("x_bf16_0", "x_bf16_1"))]
         x_codes = [keep.tile([P, V], U32, name=f"x_codes{g}", tag=tag, align_bytes=64)
                    for g, tag in enumerate(("tables6", "x_codes1"))]
         x_scales = [keep.tile([P, V], U8, name=f"x_scales{g}", align_bytes=64) for g in range(PASSES)]
@@ -104,13 +110,15 @@ def tile_picked_grid_mlp_silu_sub_l_kernel(tc, xT, w1, w2, offs, out):
                 v0, v1 = part * V // parts, (part + 1) * V // parts
                 nc.vector.tensor_copy(x_bf16[g][:, v0:v1, t], entries(level, v0, v1))
 
-        def look_up_rows(first, count):
+        def look_up_rows(first, count, interleave):
             g, t = divmod(first, PACK)
             rows = keep.tile([P, count, V], F32, name=f"x_rows{first}")
-            for i in range(count):
+            for i in range(count // 2):
                 nc.vector.tensor_copy(rows[:, i, :], entries(first + i, 0, V))
-            nc.scalar.copy(x_bf16[g][:].rearrange("p (u i) t -> p u t i", i=PACK)[:, :, t:t + count, :],
-                           rows[:].rearrange("p t (u i) -> p u t i", i=PACK))
+            for i in range(count // 2, count):
+                nc.scalar.activation(rows[:, i, :], entries(first + i, 0, V), COPY)
+            interleave(x_bf16[g][:].rearrange("p (u i) t -> p u t i", i=PACK)[:, :, t:t + count, :],
+                       rows[:].rearrange("p t (u i) -> p u t i", i=PACK))
 
         def quantize_x(g, parts=1):
             for part in range(parts):
@@ -169,31 +177,30 @@ def tile_picked_grid_mlp_silu_sub_l_kernel(tc, xT, w1, w2, offs, out):
         result = keep.tile([P, V], F32, name="result", align_bytes=64)
 
         cast_w1(0, 0, w1_early[:, :, 0:K_PASS], 0, P, on_scalar)
-        cast_w1(0, 1, w1_early[:, :, K_PASS:H - PIECE], 0, PIECE_ROWS, on_scalar)
-        look_up_rows(0, 4)
+        look_up_rows(0, 4, on_vector)
         quantize_w1(0, 0, 0, K_PASS)
-        quantize_w1_piece(0, 1, 0)
 
-        look_up_rows(4, 2)
+        look_up_rows(4, 2, on_vector)
         look_up(6)
         quantize_x(0)
         for n in range(CHUNKS):
             first_layer(0, 0, n)
         look_up(7, parts=2)
         quantize_x(1, parts=2)
-        cast_w1(0, 1, w1_rest[:], PIECE_ROWS, P, on_scalar)
-        quantize_w1_piece(0, 1, 1)
 
-        cast_w1(1, 0, w1_late[0][0][:, :, 0:PACK * SCALAR_ROWS], 0, SCALAR_ROWS, on_scalar)
-        cast_w1(1, 0, w1_late[0][0][:, :, PACK * SCALAR_ROWS:PIECE], SCALAR_ROWS, PIECE_ROWS, on_vector)
+        cast_w1(1, 0, w1_late[0][0][:], 0, PIECE_ROWS, on_scalar)
         quantize_w1_piece(1, 0, 0)
-        for tiles in TILE_PAIRS:
-            cast_w1(1, 0, w1_late[0][1][:], PIECE_ROWS, P, on_vector, tiles)
+        for tiles, copy in zip(TILE_PAIRS, (on_vector, on_scalar)):
+            cast_w1(1, 0, w1_late[0][1][:], PIECE_ROWS, P, copy, tiles)
         quantize_w1_piece(1, 0, 1)
         for n in range(CHUNKS):
             first_layer(1, 0, n)
             activate(0, n)
 
+        for piece in range(2):
+            for tiles in TILE_PAIRS:
+                cast_w1(0, 1, w1_rest[piece][:], piece * PIECE_ROWS, (piece + 1) * PIECE_ROWS, on_vector, tiles)
+            quantize_w1_piece(0, 1, piece)
         for n in range(CHUNKS):
             first_layer(0, 1, n)
         for piece in range(2):

@@ -47,25 +47,24 @@ def tile_picked_grid_mlp_silu_sub_l_kernel(tc, xT, w1, w2, offs, out):
 
         def load_tables(first, count):
             g, t = divmod(first, PACK)
-            tile = keep.tile([P, count, T], F32, name=f"tables{first}", tag=f"tables{first}", align_bytes=64)
+            tile = keep.tile([P, count, T], F32, name=f"tables{first}", tag=f"tables{first}", align_bytes=256)
             nc.sync.dma_start(out=tile[:], in_=xT_rows[g][:, t:t + count, :])
             for i in range(count):
                 tables[first + i] = tile[:, i, :]
 
         def load_w1(g, a, b):
-            tile = keep.tile([P, PACK, b - a], F32, name=f"w1_raw{g}_{a}", tag=f"w1_raw{g}_{a}", align_bytes=64)
+            tile = keep.tile([P, PACK, b - a], F32, name=f"w1_raw{g}_{a}", tag=f"w1_raw{g}_{a}", align_bytes=256)
             nc.sync.dma_start(out=tile[:], in_=w1_rows[g][:, :, a:b])
             return tile
 
-        offsets = keep.tile([P, LEVELS * LIST_COLS], U16, name="offsets")
-        w2_raw = keep.tile([P, HALVES, PACK, N], F32, name="w2_raw", tag="w2_raw", align_bytes=64)
+        offsets = keep.tile([P, LEVELS * LIST_COLS], U16, name="offsets", align_bytes=256)
+        w2_raw = keep.tile([P, HALVES, PACK, N], F32, name="w2_raw", tag="w2_raw", align_bytes=256)
         nc.sync.dma_start(offsets[:], offs)
         load_tables(0, 4)
-        w1_early = load_w1(0, 0, K_PASS)
         load_tables(4, 2)
-        for level in (6, 7):
-            load_tables(level, 1)
-        w1_late = [[load_w1(1, a, a + PIECE) for a in (0, PIECE)]]
+        load_tables(6, 2)
+        w1_early = load_w1(0, 0, K_PASS)
+        w1_late = [load_w1(1, 0, K_PASS)]
         w1_rest = [load_w1(0, K_PASS + a, K_PASS + a + PIECE) for a in (0, PIECE)]
         w1_late.append([load_w1(1, K_PASS + a, K_PASS + a + PIECE) for a in (0, PIECE)])
         nc.sync.dma_start(out=w2_raw[:], in_=w2.rearrange("(c p j) n -> p c j n", p=P, j=PACK))
@@ -98,17 +97,11 @@ def tile_picked_grid_mlp_silu_sub_l_kernel(tc, xT, w1, w2, offs, out):
         x_bf16 = [keep.tile([P, V, PACK], BF16, name=f"x_bf16_{g}", tag=tag, align_bytes=64)
                   for g, tag in enumerate(("x_bf16_0", "x_bf16_1"))]
         x_codes = [keep.tile([P, V], U32, name=f"x_codes{g}", tag=tag, align_bytes=64)
-                   for g, tag in enumerate(("tables6", "x_codes1"))]
+                   for g, tag in enumerate(("x_codes0", "x_codes1"))]
         x_scales = [keep.tile([P, V], U8, name=f"x_scales{g}", align_bytes=64) for g in range(PASSES)]
 
         def entries(level, v0, v1):
             return tables[level].indirect(offsets[:, level * LIST_COLS + v0 // 16:level * LIST_COLS + v1 // 16])
-
-        def look_up(level, parts=1):
-            g, t = divmod(level, PACK)
-            for part in range(parts):
-                v0, v1 = part * V // parts, (part + 1) * V // parts
-                nc.vector.tensor_copy(x_bf16[g][:, v0:v1, t], entries(level, v0, v1))
 
         def look_up_rows(first, count, interleave):
             g, t = divmod(first, PACK)
@@ -135,7 +128,7 @@ def tile_picked_grid_mlp_silu_sub_l_kernel(tc, xT, w1, w2, offs, out):
             quantize(w2_codes[:].rearrange("p c n -> p (c n)"), w2_scales[:].rearrange("p c n -> p (c n)"),
                      w2_bf16[:].rearrange("p c n j -> p (c n j)"))
 
-        h_bf16 = [keep.tile([P, V, PACK], BF16, name=f"h_bf16_{c}", align_bytes=64) for c in range(HALVES)]
+        h_bf16 = {1: keep.tile([P, V, PACK], BF16, name="h_bf16_1", align_bytes=64)}
         h_scales = [keep.tile([P, V], U8, name=f"h_scales{c}", align_bytes=64) for c in range(HALVES)]
         sums = {}
 
@@ -174,33 +167,42 @@ def tile_picked_grid_mlp_silu_sub_l_kernel(tc, xT, w1, w2, offs, out):
                 stop=(c == HALVES - 1),
             )
 
-        result = keep.tile([P, V], F32, name="result", align_bytes=64)
+        result = keep.tile([P, V], F32, name="result", align_bytes=256)
 
-        cast_w1(0, 0, w1_early[:, :, 0:K_PASS], 0, P, on_scalar)
         look_up_rows(0, 4, on_vector)
-        quantize_w1(0, 0, 0, K_PASS)
-
-        look_up_rows(4, 2, on_vector)
-        look_up(6)
         quantize_x(0)
+        look_up_rows(4, 2, on_vector)
+        rows = keep.tile([P, 2, V], F32, name="x_rows6")
+        halves = (slice(0, V // 2), slice(V // 2, V))
+        for v in halves:
+            nc.vector.tensor_copy(rows[:, 0, v], entries(6, v.start, v.stop))
+            nc.scalar.activation(rows[:, 1, v], entries(7, v.start, v.stop), COPY)
+        for v, copy in zip(halves, (on_vector, on_scalar)):
+            copy(x_bf16[1][:, v, :].rearrange("p (u i) t -> p u t i", i=PACK)[:, :, 2:4, :],
+                 rows[:, :, v].rearrange("p t (u i) -> p u t i", i=PACK))
+        quantize_x(1, parts=2)
+        for tiles, copy in zip(TILE_PAIRS, (on_vector, on_scalar)):
+            cast_w1(0, 0, w1_early[:], 0, P, copy, tiles)
+        for a, b in ((0, P), (P, PIECE), (PIECE, K_PASS)):
+            quantize_w1(0, 0, a, b)
         for n in range(CHUNKS):
             first_layer(0, 0, n)
-        look_up(7, parts=2)
-        quantize_x(1, parts=2)
 
-        cast_w1(1, 0, w1_late[0][0][:], 0, PIECE_ROWS, on_scalar)
-        quantize_w1_piece(1, 0, 0)
         for tiles, copy in zip(TILE_PAIRS, (on_vector, on_scalar)):
-            cast_w1(1, 0, w1_late[0][1][:], PIECE_ROWS, P, copy, tiles)
-        quantize_w1_piece(1, 0, 1)
+            cast_w1(1, 0, w1_late[0][:], 0, P, copy, tiles)
+        for a, b in ((0, PIECE), (PIECE, PIECE + P), (PIECE + P, K_PASS)):
+            quantize_w1(1, 0, a, b)
+        for tiles, copy in zip(TILE_PAIRS, (on_vector, on_scalar)):
+            cast_w1(0, 1, w1_rest[0][:], 0, PIECE_ROWS, copy, tiles)
+        h_bf16[0] = keep.tile([P, V, PACK], BF16, name="h_bf16_0", tag="w1_raw0_512", align_bytes=256)
         for n in range(CHUNKS):
             first_layer(1, 0, n)
             activate(0, n)
 
-        for piece in range(2):
-            for tiles in TILE_PAIRS:
-                cast_w1(0, 1, w1_rest[piece][:], piece * PIECE_ROWS, (piece + 1) * PIECE_ROWS, on_vector, tiles)
-            quantize_w1_piece(0, 1, piece)
+        quantize_w1_piece(0, 1, 0)
+        for tiles in TILE_PAIRS:
+            cast_w1(0, 1, w1_rest[1][:], PIECE_ROWS, P, on_vector, tiles)
+        quantize_w1_piece(0, 1, 1)
         for n in range(CHUNKS):
             first_layer(0, 1, n)
         for piece in range(2):
@@ -212,7 +214,7 @@ def tile_picked_grid_mlp_silu_sub_l_kernel(tc, xT, w1, w2, offs, out):
             activate(1, n)
 
         prepare_w2()
-        h_codes0 = keep.tile([P, V], U32, name="h_codes0", tag="w2_raw", align_bytes=64)
+        h_codes0 = keep.tile([P, V], U32, name="h_codes0", tag="w2_raw", align_bytes=256)
         quantize_h(0, h_codes0, points(0, CHUNKS))
         h_codes1 = keep.tile([P, V], U32, name="h_codes1", align_bytes=64)
         for n in range(CHUNKS):

@@ -26,6 +26,9 @@ PIECE = K_PASS // 2
 PIECE_ROWS = PIECE // PACK
 ALL_TILES = slice(0, PACK)
 TILE_PAIRS = (slice(0, 2), slice(2, 4))
+EARLY_CHUNKS = 4
+VECTOR_POINTS = 320
+AHEAD_CHUNKS = 2
 OUT_BANKS = 2
 
 
@@ -34,7 +37,7 @@ def tile_picked_grid_mlp_silu_sub_l_kernel(tc, xT, w1, w2, offs, out):
     on_vector, on_scalar = nc.vector.tensor_copy, nc.scalar.copy
     with ExitStack() as ctx:
         keep = ctx.enter_context(tc.tile_pool(name="keep", bufs=1))
-        banks = ctx.enter_context(tc.psum_pool(name="banks", bufs=8 - OUT_BANKS))
+        banks = ctx.enter_context(tc.psum_pool(name="banks", bufs=1))
         out_banks = ctx.enter_context(tc.psum_pool(name="out_banks", bufs=OUT_BANKS))
 
         warm = keep.tile([P, 2], F32, name="warm")
@@ -61,8 +64,8 @@ def tile_picked_grid_mlp_silu_sub_l_kernel(tc, xT, w1, w2, offs, out):
         w2_raw = keep.tile([P, HALVES, PACK, N], F32, name="w2_raw", tag="w2_raw", align_bytes=256)
         nc.sync.dma_start(offsets[:], offs)
         load_tables(0, 4)
-        load_tables(4, 2)
-        load_tables(6, 2)
+        load_tables(4, 3)
+        load_tables(7, 1)
         w1_early = load_w1(0, 0, K_PASS)
         w1_late = [load_w1(1, 0, K_PASS)]
         w1_rest = [load_w1(0, K_PASS + a, K_PASS + a + PIECE) for a in (0, PIECE)]
@@ -135,10 +138,16 @@ def tile_picked_grid_mlp_silu_sub_l_kernel(tc, xT, w1, w2, offs, out):
         def points(first, count=1):
             return slice(first * POINTS, (first + count) * POINTS)
 
-        def first_layer(g, c, n):
-            if g == 0:
-                sums[c, n] = banks.tile([P, PACK, POINTS], F32, name="bank")
-            for t in range(PACK):
+        done = {}
+
+        def bank_tag(c, n):
+            return f"bank{c}{n}" if n < CHUNKS - OUT_BANKS else f"bank{n}"
+
+        def first_layer(c, n, steps):
+            for g, t in steps:
+                if (c, n) not in sums:
+                    sums[c, n] = banks.tile([P, PACK, POINTS], F32, name=f"bank{c}{n}", tag=bank_tag(c, n))
+                    done[c, n] = 0
                 channels = slice(t * P, (t + 1) * P)
                 nc.tensor.matmul_mx(
                     out=sums[c, n][:, t, :],
@@ -146,9 +155,13 @@ def tile_picked_grid_mlp_silu_sub_l_kernel(tc, xT, w1, w2, offs, out):
                     lhsT_scale=w1_scales[g][c][:, channels],
                     rhs=x_codes[g][:, points(n)].bitcast(FP8X4),
                     rhs_scale=x_scales[g][:, points(n)],
-                    start=(g == 0 and t == 0),
-                    stop=(g == PASSES - 1 and t == PACK - 1),
+                    start=(done[c, n] == 0),
+                    stop=(done[c, n] == PASSES * PACK - 1),
                 )
+                done[c, n] = done[c, n] + 1
+
+        def whole_pass(g):
+            return [(g, t) for t in range(PACK)]
 
         def activate(c, n):
             nc.scalar.activation(h_bf16[c][:, points(n), :], sums[c, n][:].rearrange("p t v -> p v t"), SILU)
@@ -171,22 +184,31 @@ def tile_picked_grid_mlp_silu_sub_l_kernel(tc, xT, w1, w2, offs, out):
 
         look_up_rows(0, 4, on_vector)
         quantize_x(0)
-        look_up_rows(4, 2, on_vector)
-        rows = keep.tile([P, 2, V], F32, name="x_rows6")
-        halves = (slice(0, V // 2), slice(V // 2, V))
-        for v in halves:
-            nc.vector.tensor_copy(rows[:, 0, v], entries(6, v.start, v.stop))
-            nc.scalar.activation(rows[:, 1, v], entries(7, v.start, v.stop), COPY)
-        for v, copy in zip(halves, (on_vector, on_scalar)):
-            copy(x_bf16[1][:, v, :].rearrange("p (u i) t -> p u t i", i=PACK)[:, :, 2:4, :],
-                 rows[:, :, v].rearrange("p t (u i) -> p u t i", i=PACK))
+        rows = keep.tile([P, PACK, V], F32, name="x_rows4")
+
+        def look_up(level, v0, v1, on_scalar_engine):
+            if on_scalar_engine:
+                nc.scalar.activation(rows[:, level - PACK, v0:v1], entries(level, v0, v1), COPY)
+            else:
+                nc.vector.tensor_copy(rows[:, level - PACK, v0:v1], entries(level, v0, v1))
+
+        def interleave(copy, v0, v1):
+            copy(x_bf16[1][:, v0:v1, :].rearrange("p (u i) t -> p u t i", i=PACK),
+                 rows[:, :, v0:v1].rearrange("p t (u i) -> p u t i", i=PACK))
+
+        for level in range(PACK, LEVELS):
+            look_up(level, 0, V // 2, False)
+            look_up(level, V // 2, V, True)
+        interleave(on_vector, 0, V // 2)
+        interleave(on_vector, V // 2, VECTOR_POINTS)
+        interleave(on_scalar, VECTOR_POINTS, V)
         quantize_x(1, parts=2)
         for tiles, copy in zip(TILE_PAIRS, (on_vector, on_scalar)):
             cast_w1(0, 0, w1_early[:], 0, P, copy, tiles)
         for a, b in ((0, P), (P, PIECE), (PIECE, K_PASS)):
             quantize_w1(0, 0, a, b)
-        for n in range(CHUNKS):
-            first_layer(0, 0, n)
+        for n in range(EARLY_CHUNKS):
+            first_layer(0, n, whole_pass(0))
 
         for tiles, copy in zip(TILE_PAIRS, (on_vector, on_scalar)):
             cast_w1(1, 0, w1_late[0][:], 0, P, copy, tiles)
@@ -196,7 +218,10 @@ def tile_picked_grid_mlp_silu_sub_l_kernel(tc, xT, w1, w2, offs, out):
             cast_w1(0, 1, w1_rest[0][:], 0, PIECE_ROWS, copy, tiles)
         h_bf16[0] = keep.tile([P, V, PACK], BF16, name="h_bf16_0", tag="w1_raw0_512", align_bytes=256)
         for n in range(CHUNKS):
-            first_layer(1, 0, n)
+            steps = whole_pass(1) if n < AHEAD_CHUNKS else whole_pass(1)[::-1]
+            if n >= EARLY_CHUNKS:
+                steps = steps[:1] + whole_pass(0) + steps[1:]
+            first_layer(0, n, steps)
             activate(0, n)
 
         quantize_w1_piece(0, 1, 0)
@@ -204,13 +229,13 @@ def tile_picked_grid_mlp_silu_sub_l_kernel(tc, xT, w1, w2, offs, out):
             cast_w1(0, 1, w1_rest[1][:], PIECE_ROWS, P, on_vector, tiles)
         quantize_w1_piece(0, 1, 1)
         for n in range(CHUNKS):
-            first_layer(0, 1, n)
+            first_layer(1, n, whole_pass(0))
         for piece in range(2):
             for tiles in TILE_PAIRS:
                 cast_w1(1, 1, w1_late[1][piece][:], piece * PIECE_ROWS, (piece + 1) * PIECE_ROWS, on_vector, tiles)
             quantize_w1_piece(1, 1, piece)
         for n in range(CHUNKS):
-            first_layer(1, 1, n)
+            first_layer(1, n, whole_pass(1))
             activate(1, n)
 
         prepare_w2()

@@ -252,4 +252,4 @@ def tile_picked_grid_mlp_silu_sub_l_kernel(tc, xT, w1, w2, offs, out):
             if n == 1:
                 nc.sync.dma_start(out=out[:, points(0, 2)], in_=result[:, points(0, 2)])
             elif n > 1:
-                nc.scalar.dma_start(out=out[:, points(n)], in_=result[:, points(n)])
+                nc.sync.dma_start(out=out[:, points(n)], in_=result[:, points(n)])

@@ -235,15 +235,18 @@ def tile_picked_grid_mlp_silu_sub_l_kernel(tc, xT, w1, w2, offs, out):
                 cast_w1(1, 1, w1_late[1][piece][:], piece * PIECE_ROWS, (piece + 1) * PIECE_ROWS, on_vector, tiles)
             quantize_w1_piece(1, 1, piece)
         for n in range(CHUNKS):
-            first_layer(1, n, whole_pass(1))
+            first_layer(1, n, whole_pass(1) if n == 0 else whole_pass(1)[::-1])
             activate(1, n)
 
-        prepare_w2()
-        h_codes0 = keep.tile([P, V], U32, name="h_codes0", tag="w2_raw", align_bytes=256)
+        h_codes0 = keep.tile([P, V], U32, name="h_codes0", tag="w1_raw1_768", align_bytes=256)
         quantize_h(0, h_codes0, points(0, CHUNKS))
+        prepare_w2()
         h_codes1 = keep.tile([P, V], U32, name="h_codes1", align_bytes=64)
         for n in range(CHUNKS):
-            bank = out_banks.tile([P, V], F32, name="out_bank")
+            if n < OUT_BANKS:
+                bank = out_banks.tile([P, V], F32, name="out_bank")
+            else:
+                bank = banks.tile([P, V], F32, name=f"out_bank{n}", tag=bank_tag(0, n - OUT_BANKS))
             second_layer(0, n, h_codes0, bank)
             quantize_h(1, h_codes1, points(n))
             second_layer(1, n, h_codes1, bank)

@@ -26,9 +26,9 @@ PIECE = K_PASS // 2
 PIECE_ROWS = PIECE // PACK
 ALL_TILES = slice(0, PACK)
 TILE_PAIRS = (slice(0, 2), slice(2, 4))
-EARLY_CHUNKS = 4
+EARLY_CHUNKS = 3
 VECTOR_POINTS = 320
-AHEAD_CHUNKS = 2
+AHEAD_CHUNKS = 1
 OUT_BANKS = 2
 
 
@@ -67,9 +67,10 @@ def tile_picked_grid_mlp_silu_sub_l_kernel(tc, xT, w1, w2, offs, out):
         load_tables(4, 3)
         load_tables(7, 1)
         w1_early = load_w1(0, 0, K_PASS)
-        w1_late = [load_w1(1, 0, K_PASS)]
+        w1_late = [[load_w1(1, a, a + PIECE) for a in (0, PIECE)]]
         w1_rest = [load_w1(0, K_PASS + a, K_PASS + a + PIECE) for a in (0, PIECE)]
-        w1_late.append([load_w1(1, K_PASS + a, K_PASS + a + PIECE) for a in (0, PIECE)])
+        cuts = (K_PASS, K_PASS + PIECE, H - PIECE // 2, H)
+        w1_late.append([load_w1(1, a, b) for a, b in zip(cuts, cuts[1:])])
         nc.sync.dma_start(out=w2_raw[:], in_=w2.rearrange("(c p j) n -> p c j n", p=P, j=PACK))
 
         def quantize(codes, scales, interleaved):
@@ -141,7 +142,7 @@ def tile_picked_grid_mlp_silu_sub_l_kernel(tc, xT, w1, w2, offs, out):
         done = {}
 
         def bank_tag(c, n):
-            return f"bank{c}{n}" if n < CHUNKS - OUT_BANKS else f"bank{n}"
+            return f"bank{c}{n}" if c == 0 or n < CHUNKS - OUT_BANKS else f"bank0{n - 1}"
 
         def first_layer(c, n, steps):
             for g, t in steps:
@@ -210,10 +211,10 @@ def tile_picked_grid_mlp_silu_sub_l_kernel(tc, xT, w1, w2, offs, out):
         for n in range(EARLY_CHUNKS):
             first_layer(0, n, whole_pass(0))
 
-        for tiles, copy in zip(TILE_PAIRS, (on_vector, on_scalar)):
-            cast_w1(1, 0, w1_late[0][:], 0, P, copy, tiles)
-        for a, b in ((0, PIECE), (PIECE, PIECE + P), (PIECE + P, K_PASS)):
-            quantize_w1(1, 0, a, b)
+        for piece in range(2):
+            for tiles, copy in zip(TILE_PAIRS, (on_vector, on_scalar)):
+                cast_w1(1, 0, w1_late[0][piece][:], piece * PIECE_ROWS, (piece + 1) * PIECE_ROWS, copy, tiles)
+            quantize_w1_piece(1, 0, piece)
         for tiles, copy in zip(TILE_PAIRS, (on_vector, on_scalar)):
             cast_w1(0, 1, w1_rest[0][:], 0, PIECE_ROWS, copy, tiles)
         h_bf16[0] = keep.tile([P, V, PACK], BF16, name="h_bf16_0", tag="w1_raw0_512", align_bytes=256)
@@ -222,7 +223,8 @@ def tile_picked_grid_mlp_silu_sub_l_kernel(tc, xT, w1, w2, offs, out):
             if n >= EARLY_CHUNKS:
                 steps = steps[:1] + whole_pass(0) + steps[1:]
             first_layer(0, n, steps)
-            activate(0, n)
+            if n < CHUNKS - 1:
+                activate(0, n)
 
         quantize_w1_piece(0, 1, 0)
         for tiles in TILE_PAIRS:
@@ -230,27 +232,42 @@ def tile_picked_grid_mlp_silu_sub_l_kernel(tc, xT, w1, w2, offs, out):
         quantize_w1_piece(0, 1, 1)
         for n in range(CHUNKS):
             first_layer(1, n, whole_pass(0))
-        for piece in range(2):
-            for tiles in TILE_PAIRS:
-                cast_w1(1, 1, w1_late[1][piece][:], piece * PIECE_ROWS, (piece + 1) * PIECE_ROWS, on_vector, tiles)
-            quantize_w1_piece(1, 1, piece)
+        for tiles in TILE_PAIRS:
+            cast_w1(1, 1, w1_late[1][0][:], 0, PIECE_ROWS, on_vector, tiles)
+        quantize_w1_piece(1, 1, 0)
+        cast_w1(1, 1, w1_late[1][1][:], PIECE_ROWS, P - PIECE_ROWS // 2, on_scalar)
+        h_last = keep.tile([P, POINTS, PACK], BF16, name="h_last", tag=f"w1_raw1_{cuts[1]}", align_bytes=256)
+        nc.scalar.activation(h_last[:], sums[0, CHUNKS - 1][:].rearrange("p t v -> p v t"), SILU)
+        for tiles in TILE_PAIRS:
+            cast_w1(1, 1, w1_late[1][2][:], P - PIECE_ROWS // 2, P, on_vector, tiles)
+        quantize_w1_piece(1, 1, 1)
         for n in range(CHUNKS):
             first_layer(1, n, whole_pass(1) if n == 0 else whole_pass(1)[::-1])
-            activate(1, n)
+            if n < CHUNKS - 1:
+                activate(1, n)
+        last_halves = [slice(a, a + POINTS // 2) for a in (0, POINTS // 2)]
+        for v in last_halves:
+            nc.scalar.activation(h_bf16[1][:, points(CHUNKS - 1), :][:, v, :],
+                                 sums[1, CHUNKS - 1][:].rearrange("p t v -> p v t")[:, v, :], SILU)
 
-        h_codes0 = keep.tile([P, V], U32, name="h_codes0", tag="w1_raw1_768", align_bytes=256)
-        quantize_h(0, h_codes0, points(0, CHUNKS))
+        h_codes0 = keep.tile([P, V], U32, name="h_codes0", tag=f"w1_raw1_{cuts[2]}", align_bytes=256)
+        quantize_h(0, h_codes0, points(0, CHUNKS - 1))
+        quantize(h_codes0[:, points(CHUNKS - 1)], h_scales[0][:, points(CHUNKS - 1)], h_last[:].rearrange("p v t -> p (v t)"))
         prepare_w2()
         h_codes1 = keep.tile([P, V], U32, name="h_codes1", align_bytes=64)
         for n in range(CHUNKS):
             if n < OUT_BANKS:
                 bank = out_banks.tile([P, V], F32, name="out_bank")
             else:
-                bank = banks.tile([P, V], F32, name=f"out_bank{n}", tag=bank_tag(0, n - OUT_BANKS))
+                bank = banks.tile([P, V], F32, name=f"out_bank{n}", tag=bank_tag(0, (CHUNKS - 1) * (n - OUT_BANKS)))
             second_layer(0, n, h_codes0, bank)
-            quantize_h(1, h_codes1, points(n))
+            if n < CHUNKS - 1:
+                quantize_h(1, h_codes1, points(n))
+            else:
+                for v in last_halves:
+                    quantize_h(1, h_codes1, slice(n * POINTS + v.start, n * POINTS + v.stop))
             second_layer(1, n, h_codes1, bank)
-            copy = on_vector if n == 0 else on_scalar
+            copy = on_vector if n in (0, CHUNKS - 1) else on_scalar
             copy(result[:, points(n)], bank[:, 0:POINTS])
             if n == 1:
                 nc.sync.dma_start(out=out[:, points(0, 2)], in_=result[:, points(0, 2)])

@@ -62,8 +62,8 @@ def tile_picked_grid_mlp_silu_sub_l_kernel(tc, xT, w1, w2, offs, out):
 
         offsets = keep.tile([P, LEVELS * LIST_COLS], U16, name="offsets", align_bytes=256)
         w2_raw = keep.tile([P, HALVES, PACK, N], F32, name="w2_raw", tag="w2_raw", align_bytes=256)
-        nc.sync.dma_start(offsets[:], offs)
         load_tables(0, 4)
+        nc.sync.dma_start(offsets[:], offs)
         load_tables(4, 3)
         load_tables(7, 1)
         w1_early = load_w1(0, 0, K_PASS)

from contextlib import ExitStack

import concourse.mybir as mybir

K, T, LEVELS, V, H, N = 1024, 2048, 8, 512, 1024, 128
FLOPS = 2 * K * H * V + 2 * H * N * V

F32 = mybir.dt.float32
BF16 = mybir.dt.bfloat16
U32 = mybir.dt.uint32
U16 = mybir.dt.uint16
U8 = mybir.dt.uint8
FP8X4 = mybir.dt.float8_e4m3fn_x4
SILU = mybir.ActivationFunctionType.Silu
COPY = mybir.ActivationFunctionType.Copy

P = 128
PACK = 4
K_PASS = P * PACK
PASSES = K // K_PASS
HALVES = H // K_PASS
POINTS = 128
CHUNKS = V // POINTS
LIST_COLS = V // 16
PIECE = K_PASS // 2
PIECE_ROWS = PIECE // PACK
ALL_TILES = slice(0, PACK)
TILE_PAIRS = (slice(0, 2), slice(2, 4))
EARLY_CHUNKS = 3
VECTOR_POINTS = 320
AHEAD_CHUNKS = 1
OUT_BANKS = 2


def tile_picked_grid_mlp_silu_sub_l_kernel(tc, xT, w1, w2, offs, out):
    nc = tc.nc
    on_vector, on_scalar = nc.vector.tensor_copy, nc.scalar.copy
    with ExitStack() as ctx:
        keep = ctx.enter_context(tc.tile_pool(name="keep", bufs=1))
        banks = ctx.enter_context(tc.psum_pool(name="banks", bufs=1))
        out_banks = ctx.enter_context(tc.psum_pool(name="out_banks", bufs=OUT_BANKS))

        warm = keep.tile([P, 2], F32, name="warm")
        nc.gpsimd.memset(warm[:, 0:1], 0.0)
        nc.scalar.activation(warm[:, 1:2], warm[:, 0:1], SILU)

        w1_rows = [w1[g * K_PASS:(g + 1) * K_PASS, :].rearrange("(p j) w -> p j w", j=PACK) for g in range(PASSES)]
        xT_rows = [xT[g * K_PASS:(g + 1) * K_PASS, :].rearrange("(p t) w -> p t w", t=PACK) for g in range(PASSES)]
        tables = {}

        def load_tables(first, count):
            g, t = divmod(first, PACK)
            tile = keep.tile([P, count, T], F32, name=f"tables{first}", tag=f"tables{first}", align_bytes=256)
            nc.sync.dma_start(out=tile[:], in_=xT_rows[g][:, t:t + count, :])
            for i in range(count):
                tables[first + i] = tile[:, i, :]

        def load_w1(g, a, b):
            tile = keep.tile([P, PACK, b - a], F32, name=f"w1_raw{g}_{a}", tag=f"w1_raw{g}_{a}", align_bytes=256)
            nc.sync.dma_start(out=tile[:], in_=w1_rows[g][:, :, a:b])
            return tile

        offsets = keep.tile([P, LEVELS * LIST_COLS], U16, name="offsets", align_bytes=256)
        w2_raw = keep.tile([P, HALVES, PACK, N], F32, name="w2_raw", tag="w2_raw", align_bytes=256)
        load_tables(0, 4)
        nc.sync.dma_start(offsets[:], offs)
        load_tables(4, 3)
        load_tables(7, 1)
        w1_early = load_w1(0, 0, K_PASS)
        w1_late = [[load_w1(1, a, a + PIECE) for a in (0, PIECE)]]
        w1_rest = [load_w1(0, K_PASS + a, K_PASS + a + PIECE) for a in (0, PIECE)]
        cuts = (K_PASS, K_PASS + PIECE, H - PIECE // 2, H)
        w1_late.append([load_w1(1, a, b) for a, b in zip(cuts, cuts[1:])])
        nc.sync.dma_start(out=w2_raw[:], in_=w2.rearrange("(c p j) n -> p c j n", p=P, j=PACK))

        def quantize(codes, scales, interleaved):
            nc.vector.quantize_mx(out=codes.bitcast(FP8X4), scales=scales, in_=interleaved)

        def w1_tiles(kind, width, dtype):
            return [[keep.tile([P, width], dtype, name=f"w1_{kind}{g}{c}", tag=f"w1_{kind}{g}{c}", align_bytes=64)
                     for c in range(HALVES)] for g in range(PASSES)]

        w1_bf16 = w1_tiles("bf16_", K_PASS * PACK, BF16)
        w1_codes = w1_tiles("codes", K_PASS, U32)
        w1_scales = w1_tiles("scales", K_PASS, U8)

        def cast_w1(g, c, raw, m0, m1, copy, tiles=ALL_TILES):
            copy(
                out=w1_bf16[g][c][:].rearrange("p (t m j) -> p m j t", t=PACK, j=PACK)[:, m0:m1, :, tiles],
                in_=raw.rearrange("p j (m t) -> p m j t", t=PACK)[:, :, :, tiles],
            )

        def quantize_w1(g, c, a, b):
            quantize(w1_codes[g][c][:, a:b], w1_scales[g][c][:, a:b], w1_bf16[g][c][:, PACK * a:PACK * b])

        def quantize_w1_piece(g, c, piece):
            for t in range(PACK):
                a = t * P + piece * PIECE_ROWS
                quantize_w1(g, c, a, a + PIECE_ROWS)

        x_bf16 = [keep.tile([P, V, PACK], BF16, name=f"x_bf16_{g}", tag=tag, align_bytes=64)
                  for g, tag in enumerate(("x_bf16_0", "x_bf16_1"))]
        x_codes = [keep.tile([P, V], U32, name=f"x_codes{g}", tag=tag, align_bytes=64)
                   for g, tag in enumerate(("x_codes0", "x_codes1"))]
        x_scales = [keep.tile([P, V], U8, name=f"x_scales{g}", align_bytes=64) for g in range(PASSES)]

        def entries(level, v0, v1):
            return tables[level].indirect(offsets[:, level * LIST_COLS + v0 // 16:level * LIST_COLS + v1 // 16])

        def look_up_rows(first, count, interleave):
            g, t = divmod(first, PACK)
            rows = keep.tile([P, count, V], F32, name=f"x_rows{first}")
            for i in range(count // 2):
                nc.vector.tensor_copy(rows[:, i, :], entries(first + i, 0, V))
            for i in range(count // 2, count):
                nc.scalar.activation(rows[:, i, :], entries(first + i, 0, V), COPY)
            interleave(x_bf16[g][:].rearrange("p (u i) t -> p u t i", i=PACK)[:, :, t:t + count, :],
                       rows[:].rearrange("p t (u i) -> p u t i", i=PACK))

        def quantize_x(g, parts=1):
            for part in range(parts):
                v = slice(part * V // parts, (part + 1) * V // parts)
                quantize(x_codes[g][:, v], x_scales[g][:, v], x_bf16[g][:, v, :].rearrange("p v t -> p (v t)"))

        w2_codes = keep.tile([P, HALVES, N], U32, name="w2_codes", align_bytes=64)
        w2_scales = keep.tile([P, HALVES, N], U8, name="w2_scales", align_bytes=64)

        def prepare_w2():
            w2_bf16 = keep.tile([P, HALVES, N, PACK], BF16, name="w2_bf16", tag="w1_bf16_11", align_bytes=64)
            nc.vector.tensor_copy(w2_bf16[:].rearrange("p c (u i) j -> p c u j i", i=PACK),
                                  w2_raw[:].rearrange("p c j (u i) -> p c u j i", i=PACK))
            quantize(w2_codes[:].rearrange("p c n -> p (c n)"), w2_scales[:].rearrange("p c n -> p (c n)"),
                     w2_bf16[:].rearrange("p c n j -> p (c n j)"))

        h_bf16 = {1: keep.tile([P, V, PACK], BF16, name="h_bf16_1", align_bytes=64)}
        h_scales = [keep.tile([P, V], U8, name=f"h_scales{c}", align_bytes=64) for c in range(HALVES)]
        sums = {}

        def points(first, count=1):
            return slice(first * POINTS, (first + count) * POINTS)

        done = {}

        def bank_tag(c, n):
            return f"bank{c}{n}" if c == 0 or n < CHUNKS - OUT_BANKS else f"bank0{n - 1}"

        def first_layer(c, n, steps):
            for g, t in steps:
                if (c, n) not in sums:
                    sums[c, n] = banks.tile([P, PACK, POINTS], F32, name=f"bank{c}{n}", tag=bank_tag(c, n))
                    done[c, n] = 0
                channels = slice(t * P, (t + 1) * P)
                nc.tensor.matmul_mx(
                    out=sums[c, n][:, t, :],
                    lhsT=w1_codes[g][c][:, channels].bitcast(FP8X4),
                    lhsT_scale=w1_scales[g][c][:, channels],
                    rhs=x_codes[g][:, points(n)].bitcast(FP8X4),
                    rhs_scale=x_scales[g][:, points(n)],
                    start=(done[c, n] == 0),
                    stop=(done[c, n] == PASSES * PACK - 1),
                )
                done[c, n] = done[c, n] + 1

        def whole_pass(g):
            return [(g, t) for t in range(PACK)]

        def activate(c, n):
            nc.scalar.activation(h_bf16[c][:, points(n), :], sums[c, n][:].rearrange("p t v -> p v t"), SILU)

        def quantize_h(c, codes, v):
            quantize(codes[:, v], h_scales[c][:, v], h_bf16[c][:, v, :].rearrange("p v t -> p (v t)"))

        def second_layer(c, n, codes, bank):
            nc.tensor.matmul_mx(
                out=bank[:, 0:POINTS],
                lhsT=w2_codes[:, c, :].bitcast(FP8X4),
                lhsT_scale=w2_scales[:, c, :],
                rhs=codes[:, points(n)].bitcast(FP8X4),
                rhs_scale=h_scales[c][:, points(n)],
                start=(c == 0),
                stop=(c == HALVES - 1),
            )

        result = keep.tile([P, V], F32, name="result", align_bytes=256)

        look_up_rows(0, 4, on_vector)
        quantize_x(0)
        rows = keep.tile([P, PACK, V], F32, name="x_rows4")

        def look_up(level, v0, v1, on_scalar_engine):
            if on_scalar_engine:
                nc.scalar.activation(rows[:, level - PACK, v0:v1], entries(level, v0, v1), COPY)
            else:
                nc.vector.tensor_copy(rows[:, level - PACK, v0:v1], entries(level, v0, v1))

        def interleave(copy, v0, v1):
            copy(x_bf16[1][:, v0:v1, :].rearrange("p (u i) t -> p u t i", i=PACK),
                 rows[:, :, v0:v1].rearrange("p t (u i) -> p u t i", i=PACK))

        for level in range(PACK, LEVELS):
            look_up(level, 0, V // 2, False)
            look_up(level, V // 2, V, True)
        interleave(on_vector, 0, V // 2)
        interleave(on_vector, V // 2, VECTOR_POINTS)
        interleave(on_scalar, VECTOR_POINTS, V)
        quantize_x(1, parts=2)
        for tiles, copy in zip(TILE_PAIRS, (on_vector, on_scalar)):
            cast_w1(0, 0, w1_early[:], 0, P, copy, tiles)
        for a, b in ((0, P), (P, PIECE), (PIECE, K_PASS)):
            quantize_w1(0, 0, a, b)
        for n in range(EARLY_CHUNKS):
            first_layer(0, n, whole_pass(0))

        for piece in range(2):
            for tiles, copy in zip(TILE_PAIRS, (on_vector, on_scalar)):
                cast_w1(1, 0, w1_late[0][piece][:], piece * PIECE_ROWS, (piece + 1) * PIECE_ROWS, copy, tiles)
            quantize_w1_piece(1, 0, piece)
        for tiles, copy in zip(TILE_PAIRS, (on_vector, on_scalar)):
            cast_w1(0, 1, w1_rest[0][:], 0, PIECE_ROWS, copy, tiles)
        h_bf16[0] = keep.tile([P, V, PACK], BF16, name="h_bf16_0", tag="w1_raw0_512", align_bytes=256)
        for n in range(CHUNKS):
            steps = whole_pass(1) if n < AHEAD_CHUNKS else whole_pass(1)[::-1]
            if n >= EARLY_CHUNKS:
                steps = steps[:1] + whole_pass(0) + steps[1:]
            first_layer(0, n, steps)
            if n < CHUNKS - 1:
                activate(0, n)

        quantize_w1_piece(0, 1, 0)
        for tiles in TILE_PAIRS:
            cast_w1(0, 1, w1_rest[1][:], PIECE_ROWS, P, on_vector, tiles)
        quantize_w1_piece(0, 1, 1)
        for n in range(CHUNKS):
            first_layer(1, n, whole_pass(0))
        for tiles in TILE_PAIRS:
            cast_w1(1, 1, w1_late[1][0][:], 0, PIECE_ROWS, on_vector, tiles)
        quantize_w1_piece(1, 1, 0)
        cast_w1(1, 1, w1_late[1][1][:], PIECE_ROWS, P - PIECE_ROWS // 2, on_scalar)
        h_last = keep.tile([P, POINTS, PACK], BF16, name="h_last", tag=f"w1_raw1_{cuts[1]}", align_bytes=256)
        nc.scalar.activation(h_last[:], sums[0, CHUNKS - 1][:].rearrange("p t v -> p v t"), SILU)
        for tiles in TILE_PAIRS:
            cast_w1(1, 1, w1_late[1][2][:], P - PIECE_ROWS // 2, P, on_vector, tiles)
        quantize_w1_piece(1, 1, 1)
        for n in range(CHUNKS):
            first_layer(1, n, whole_pass(1) if n == 0 else whole_pass(1)[::-1])
            if n < CHUNKS - 1:
                activate(1, n)
        last_halves = [slice(a, a + POINTS // 2) for a in (0, POINTS // 2)]
        for v in last_halves:
            nc.scalar.activation(h_bf16[1][:, points(CHUNKS - 1), :][:, v, :],
                                 sums[1, CHUNKS - 1][:].rearrange("p t v -> p v t")[:, v, :], SILU)

        h_codes0 = keep.tile([P, V], U32, name="h_codes0", tag=f"w1_raw1_{cuts[2]}", align_bytes=256)
        quantize_h(0, h_codes0, points(0, CHUNKS - 1))
        quantize(h_codes0[:, points(CHUNKS - 1)], h_scales[0][:, points(CHUNKS - 1)], h_last[:].rearrange("p v t -> p (v t)"))
        prepare_w2()
        h_codes1 = keep.tile([P, V], U32, name="h_codes1", align_bytes=64)
        for n in range(CHUNKS):
            if n < OUT_BANKS:
                bank = out_banks.tile([P, V], F32, name="out_bank")
            else:
                bank = banks.tile([P, V], F32, name=f"out_bank{n}", tag=bank_tag(0, (CHUNKS - 1) * (n - OUT_BANKS)))
            second_layer(0, n, h_codes0, bank)
            if n < CHUNKS - 1:
                quantize_h(1, h_codes1, points(n))
            else:
                for v in last_halves:
                    quantize_h(1, h_codes1, slice(n * POINTS + v.start, n * POINTS + v.stop))
            second_layer(1, n, h_codes1, bank)
            copy = on_vector if n in (0, CHUNKS - 1) else on_scalar
            copy(result[:, points(n)], bank[:, 0:POINTS])
            if n == 1:
                nc.sync.dma_start(out=out[:, points(0, 2)], in_=result[:, points(0, 2)])
            elif n > 1:
                nc.sync.dma_start(out=out[:, points(n)], in_=result[:, points(n)])
